import numpy as np
import ml_dtypes


def mxq(x, axis, fmt="e4m3"):
    dtype, down = {"e4m3": (ml_dtypes.float8_e4m3fn, 7), "e5m2": (ml_dtypes.float8_e5m2, 14)}[fmt]
    v = np.moveaxis(np.asarray(x, np.float32).astype(ml_dtypes.bfloat16).astype(np.float64), axis, -1)
    blocks = v.reshape(v.shape[:-1] + (-1, 32))
    amax = np.abs(blocks).max(-1, keepdims=True)
    byte = np.maximum(np.where(amax > 0, np.frexp(amax)[1] - 1 + 127, 0) - down, 1)
    scale = np.exp2(byte - 127.0)
    codes = (blocks / scale).astype(np.float32).astype(dtype).astype(np.float64)
    return np.moveaxis((codes * scale).reshape(v.shape), -1, axis)


WIDE = False


def mx_kscale(k):
    if not WIDE:
        return np.ones(k)
    levels = np.array([10, -10, 5, -5, 0])
    if k % 512:
        return np.exp2(np.random.permutation(np.resize(levels, k // 32))).repeat(32)
    a = np.empty((k // 512, 16))
    for p in range(k // 512):
        a[p, :8] = np.random.permutation(np.resize(levels, 8))
        for g in range(8):
            far = levels[np.abs(levels - a[p, g]) >= 10]
            a[p, g + 8] = far[np.random.randint(len(far))]
    return np.exp2(a.ravel()).repeat(32)


BF16 = ml_dtypes.bfloat16


def bf(x):
    return np.asarray(x, np.float32).astype(BF16)


def f64(x):
    return np.asarray(x).astype(np.float64)


E2M1 = np.array([0.0, 0.5, 1.0, 1.5, 2.0, 3.0, 4.0, 6.0, -0.0, -0.5, -1.0, -1.5, -2.0, -3.0, -4.0, -6.0])


def pack_weight(w, fmt):
    k, n = w.shape
    w = f64(bf(w)).reshape(k // 32, 32, n)
    amax = np.abs(w).max(1)
    if fmt == "e4m3":
        byte = np.frexp(amax)[1] - 1 + 127 - 7
    else:
        mant, ex = np.frexp(amax / 6.0)
        byte = np.where(mant > 0.5, ex, ex - 1) + 127
    byte = np.clip(np.where(amax > 0, byte, 1), 1, 254)
    scaled = (w * np.exp2(127.0 - byte)[:, None, :]).reshape(k, n).astype(np.float32)
    by_word = np.ascontiguousarray(scaled.reshape(k // 512, 128, 4, n).transpose(0, 1, 3, 2))
    if fmt == "e4m3":
        words = by_word.astype(ml_dtypes.float8_e4m3fn).view(np.uint8)
    else:
        c = by_word.astype(ml_dtypes.float4_e2m1fn).view(np.uint8) & 0xF
        words = c[..., 0::2] | (c[..., 1::2] << 4)
    return np.ascontiguousarray(words), np.ascontiguousarray(byte.astype(np.uint8).reshape(k // 512, 16, n))


def unpack_weight(words, scales, fmt):
    g, p, n, _ = words.shape
    if fmt == "e4m3":
        vals = np.ascontiguousarray(words).view(ml_dtypes.float8_e4m3fn).astype(np.float64)
    else:
        nib = np.empty((g, p, n, 4), np.uint8)
        nib[..., 0::2] = words & 0xF
        nib[..., 1::2] = words >> 4
        vals = E2M1[nib]
    vals = vals * np.repeat(np.exp2(scales.astype(np.float64) - 127.0), 8, axis=1)[..., None]
    return vals.transpose(0, 1, 3, 2).reshape(g * 512, n)
def pack4(w):
    words, scales = pack_weight(w, "e2m1")
    return words.reshape(words.shape[0], 128, -1), scales


def unpack4(words, scales):
    return unpack_weight(words.reshape(words.shape[0], 128, -1, 2), scales, "e2m1")


def planes(Y):
    n, m = Y.shape
    b = f64(bf(Y)).reshape(n // 32, 32, m)
    amax = np.abs(b).max(1)
    byte = np.clip(np.where(amax > 0, np.frexp(amax)[1] - 1 + 127 - 7, 1), 1, 254)
    codes = (b * np.exp2(127.0 - byte)[:, None, :]).reshape(n, m).astype(np.float32).astype(ml_dtypes.float8_e4m3fn).view(np.uint8)
    words = codes.reshape(n // 512, 128, 4, m).transpose(0, 1, 3, 2)
    return np.ascontiguousarray(words), np.ascontiguousarray(byte.astype(np.uint8).reshape(n // 512, 16, m))


G, T, E, P, N = 4, 512, 1024, 1536, 512

def setup_inputs():
    s = mx_kscale(G * E)
    t = mx_kscale(G * P)
    vref = np.exp(0.3 * np.random.randn(G, E))
    dv = np.random.randn(G, T, E) * vref[:, None, :] * s.reshape(G, 1, E)
    R = np.random.randn(G * E, P) / np.sqrt(E) / s[:, None]
    gain = (1 + 0.1 * np.random.randn(G, P)) * t.reshape(G, P)
    C = 1.6 * np.random.randn(G * P, N) / np.sqrt(P) / t[:, None]
    r_words, r_scales = pack4(R)
    c_words, c_scales = pack4(C)
    rest = 0.4 * np.random.randn(G, N)
    stiff = np.exp(0.7 * np.random.randn(G, N))
    return {"dv": bf(dv), "vref": bf(vref), "r_words": r_words, "r_scales": r_scales,
            "gain": bf(gain), "c_words": c_words, "c_scales": c_scales,
            "rest": bf(rest), "stiff": bf(stiff)}

def reference(dv, vref, r_words, r_scales, gain, c_words, c_scales, rest, stiff):
    R = unpack4(r_words, r_scales).reshape(G, E, P)
    C = unpack4(c_words, c_scales).reshape(G, P, N)
    X = f64(dv) / f64(vref)[:, None, :]
    S = mxq(X, 2, "e4m3") @ R
    H = np.tanh(S) * f64(gain)[:, None, :]
    Z = mxq(H, 2, "e4m3") @ C
    y = (Z + f64(rest)[:, None, :]) * f64(stiff)[:, None, :]
    Y = y.transpose(2, 0, 1).reshape(N, G * T)
    words, scales = planes(Y)
    return y, words, scales

@@ -1,0 +1,368 @@
+from contextlib import ExitStack
+
+import concourse.mybir as mybir
+from concourse.masks import make_identity
+
+G, T, E, PX, N = 4, 512, 1024, 1536, 512
+FLOPS = 2 * G * T * (E * PX + PX * N)
+
+F32 = mybir.dt.float32
+BF16 = mybir.dt.bfloat16
+I32 = mybir.dt.int32
+U32 = mybir.dt.uint32
+U8 = mybir.dt.uint8
+FP8X4 = mybir.dt.float8_e4m3fn_x4
+FP4X4 = mybir.dt.float4_e2m1fn_x4
+ALU = mybir.AluOpType
+ACT = mybir.ActivationFunctionType
+
+P = 128
+KP = 512
+GE = E // KP
+GP = PX // KP
+TILES = T // P
+UNITS = G * TILES
+
+
+def tile_tactile_impedance_patches_k7_kernel(
+    tc, dv, vref, r_words, r_scales, gain, c_words, c_scales, rest, stiff, out_0, out_1, out_2
+):
+    nc = tc.nc
+    with ExitStack() as ctx:
+        keep = ctx.enter_context(tc.tile_pool(name="keep", bufs=1))
+        work = ctx.enter_context(tc.tile_pool(name="work", bufs=2))
+        psum = ctx.enter_context(tc.psum_pool(name="psum", bufs=1))
+        ctx.enter_context(tc.manual_schedule())
+
+        ident = keep.tile([P, P], F32, name="ident")
+        make_identity(nc, ident[:])
+        warm = keep.tile([P, 8], F32, name="warm")
+        nc.vector.memset(warm[:, 0:1], 0.0)
+        nc.scalar.activation(out=warm[:, 4:5], in_=warm[:, 0:1], func=ACT.Tanh)
+
+        r_planes, c_planes = [], []
+        for a in range(G):
+            r_planes.append(keep.tile([P, GE, PX], U8, name="r_plane%d" % a, align_bytes=64))
+            c_planes.append(keep.tile([P, GP, N], U8, name="c_plane%d" % a, align_bytes=64))
+        for a in range(G):
+            nc.vector.memset(r_planes[a][:].rearrange("p g n -> p (g n)").bitcast(I32), 0)
+            nc.vector.memset(c_planes[a][:].rearrange("p g n -> p (g n)").bitcast(I32), 0)
+
+        dv_sb, r_sb, c_sb, gain_sb, rest_sb, stiff_sb, recip = {}, {}, {}, {}, {}, {}, {}
+
+        def load_dv(i):
+            a, j = divmod(i, TILES)
+            dv_sb[i] = work.tile([P, E], BF16, name="dv_t", bufs=5)
+            nc.sync.dma_start(out=dv_sb[i][:], in_=dv[a, j * P:(j + 1) * P, :])
+
+        def load_vref(a):
+            v = keep.tile([P, GE, 16], BF16, name="vref%d" % a)
+            with nc.allow_non_contiguous_dma("four values a partition and group"):
+                nc.sync.dma_start(out=v[:, :, 0:4], in_=vref[a].rearrange("(g p t) -> p g t", g=GE, t=4))
+            recip[a] = keep.tile([P, GE, 4], F32, name="recip%d" % a)
+            return v
+
+        def load_scales(plane, scales, groups):
+            for q in range(4):
+                nc.sync.dma_start(
+                    out=plane[32 * q:32 * q + 4, :, :].bitcast(I32),
+                    in_=scales[groups, 4 * q:4 * q + 4, :].rearrange("g r n -> r g n").bitcast(I32),
+                )
+
+        def load_r(a, c):
+            r_sb[a, c] = keep.tile([P, GE, 2 * KP], U8, name="r%d_%d" % (a, c), align_bytes=64)
+            nc.sync.dma_start(
+                out=r_sb[a, c][:].bitcast(I32),
+                in_=r_words[GE * a:GE * (a + 1), :, 2 * KP * c:2 * KP * (c + 1)].rearrange("g p n -> p g n").bitcast(I32),
+            )
+
+        def load_gain(a):
+            gain_sb[a] = keep.tile([P, PX], BF16, name="gain%d" % a)
+            nc.sync.dma_start(out=gain_sb[a][:], in_=gain[a].partition_broadcast(P))
+
+        def load_c(a):
+            load_scales(c_planes[a], c_scales, slice(GP * a, GP * (a + 1)))
+            c_sb[a] = keep.tile([P, GP, 2 * N], U8, name="c%d" % a, align_bytes=64)
+            nc.sync.dma_start(
+                out=c_sb[a][:].bitcast(I32),
+                in_=c_words[GP * a:GP * (a + 1)].rearrange("g p n -> p g n").bitcast(I32),
+            )
+
+        def load_rest(a):
+            rest_sb[a] = keep.tile([P, N], BF16, name="rest%d" % a)
+            nc.sync.dma_start(out=rest_sb[a][:], in_=rest[a].partition_broadcast(P))
+            stiff_sb[a] = keep.tile([P, N], BF16, name="stiff%d" % a)
+            nc.sync.dma_start(out=stiff_sb[a][:], in_=stiff[a].partition_broadcast(P))
+
+        x_ps, x_bf, x_q, x_s, s_ps, th, h_bf = {}, {}, {}, {}, {}, {}, {}
+        h_qa, h_sa, h_qb, h_sb, z_ps, y_sb, y_bf, y_s = {}, {}, {}, {}, {}, {}, {}, {}
+        offs = {}
+
+        def live(i):
+            return 0 <= i < UNITS
+
+        def turn_x(i):
+            x_ps[i] = psum.tile([P, 2 * GE, P], F32, name="x_ps", bufs=2)
+            words = dv_sb[i][:].bitcast(F32)
+            for g in range(GE):
+                for u in range(2):
+                    nc.tensor.transpose(x_ps[i][:, 2 * g + u, :], words[:, 256 * g + u:256 * (g + 1):2], ident[:])
+
+        def divide_x(i):
+            a = i // TILES
+            x_bf[i] = work.tile([P, E], BF16, name="x_bf", align_bytes=64)
+            for g in range(GE):
+                nc.vector.tensor_tensor(
+                    out=x_bf[i][:, KP * g:KP * (g + 1)].rearrange("p (r u e) -> p r u e", u=2, e=2),
+                    in0=x_ps[i][:, 2 * g:2 * g + 2, :].bitcast(BF16).rearrange("p u (r e) -> p r u e", e=2),
+                    in1=recip[a][:, g, :].rearrange("p (u e) -> p u e", e=2).unsqueeze(1).to_broadcast([P, P, 2, 2]),
+                    op=ALU.mult,
+                )
+
+        def quantize_x(i):
+            x_q[i] = work.tile([P, GE * P], U32, name="x_q", align_bytes=64, bufs=3)
+            x_s[i] = work.tile([P, GE * P], U8, name="x_s", align_bytes=64, bufs=3)
+            nc.vector.quantize_mx(out=x_q[i][:].bitcast(FP8X4), scales=x_s[i][:], in_=x_bf[i][:])
+
+        def stage1(i):
+            a = i // TILES
+            for c in range(GP):
+                s_ps[i, c] = psum.tile([P, KP], F32, name="s_ps%d" % c)
+                for g in range(GE):
+                    nc.tensor.matmul_mx(
+                        out=s_ps[i, c][:],
+                        lhsT=x_q[i][:, P * g:P * (g + 1)].bitcast(FP8X4),
+                        lhsT_scale=x_s[i][:, P * g:P * (g + 1)],
+                        rhs=r_sb[a, c][:, g, :].bitcast(FP4X4),
+                        rhs_scale=r_planes[a][:, g, KP * c:KP * (c + 1)],
+                        start=(g == 0),
+                        stop=(g == GE - 1),
+                    )
+
+        def saturate(i):
+            for c in range(GP):
+                th[i, c] = work.tile([P, KP], F32, name="th%d" % c, bufs=4 if c == GP - 1 else 2)
+                nc.scalar.activation(
+                    out=th[i, c][:].rearrange("p (u m e) -> p u m e", u=2, e=2),
+                    in_=s_ps[i, c][:].rearrange("p (m u e) -> p u m e", u=2, e=2),
+                    func=ACT.Tanh,
+                )
+
+        def apply_gain(i):
+            a = i // TILES
+            for c in range(GP):
+                h_bf[i, c] = work.tile([P, KP], BF16, name="h_bf%d" % c)
+                nc.vector.tensor_tensor(
+                    out=h_bf[i, c][:].rearrange("p (u m e) -> p u m e", u=2, e=2),
+                    in0=th[i, c][:].rearrange("p (u m e) -> p u m e", u=2, e=2),
+                    in1=gain_sb[a][:, KP * c:KP * (c + 1)].rearrange("p (m u e) -> p u m e", u=2, e=2),
+                    op=ALU.mult,
+                )
+
+        def turn_words(bank, slot, src):
+            words = src[:].bitcast(F32)
+            for u in range(2):
+                nc.tensor.transpose(bank[:, 2 * slot + u, :], words[:, P * u:P * (u + 1)], ident[:])
+
+        def copy_words(dst, bank, lo, hi):
+            nc.scalar.copy(
+                out=dst[:, KP * lo:KP * hi].bitcast(F32).rearrange("p (g r u) -> p g r u", r=P, u=2),
+                in_=bank[:, 2 * lo:2 * hi, :].rearrange("p (g u) r -> p g r u", u=2),
+            )
+
+        def stage2(i, tag):
+            a = i // TILES
+            z_ps[i] = psum.tile([P, N], F32, name=tag)
+            for g in range(GP):
+                codes, scales, col = (h_qa[i], h_sa[i], g) if g < 2 else (h_qb[i], h_sb[i], 0)
+                nc.tensor.matmul_mx(
+                    out=z_ps[i][:],
+                    lhsT=codes[:, P * col:P * (col + 1)].bitcast(FP8X4),
+                    lhsT_scale=scales[:, P * col:P * (col + 1)],
+                    rhs=c_sb[a][:, g, :].bitcast(FP4X4),
+                    rhs_scale=c_planes[a][:, g, :],
+                    start=(g == 0),
+                    stop=(g == GP - 1),
+                )
+
+        def add_rest(i):
+            offs[i] = work.tile([P, N], F32, name="offs", bufs=4)
+            nc.vector.tensor_tensor(out=offs[i][:], in0=z_ps[i][:], in1=rest_sb[i // TILES][:], op=ALU.add)
+
+        def apply_stiff(i, eng, dst):
+            a, j = divmod(i, TILES)
+            y_sb[i] = dst
+            eng.tensor_tensor(out=dst[:], in0=offs[i][:], in1=stiff_sb[a][:], op=ALU.mult)
+            nc.sync.dma_start(out=out_0[a, j * P:(j + 1) * P, :], in_=dst[:])
+
+        def stiff_to_words(i):
+            y_bf[i] = work.tile([P, N], BF16, name="y_bf", bufs=3)
+            nc.vector.tensor_tensor(
+                out=y_bf[i][:].rearrange("p (u m e) -> p u m e", u=2, e=2),
+                in0=offs[i][:].rearrange("p (m u e) -> p u m e", u=2, e=2),
+                in1=stiff_sb[i // TILES][:].rearrange("p (m u e) -> p u m e", u=2, e=2),
+                op=ALU.mult,
+            )
+
+        def round_y(i):
+            y_bf[i] = work.tile([P, N], BF16, name="y_bf", bufs=3)
+            nc.scalar.copy(
+                out=y_bf[i][:].rearrange("p (u m e) -> p u m e", u=2, e=2),
+                in_=y_sb[i][:].rearrange("p (m u e) -> p u m e", u=2, e=2),
+            )
+
+        def quantize_y(i, src):
+            a, j = divmod(i, TILES)
+            if j == 0:
+                y_s[a] = work.tile([P, T], U8, name="y_s", align_bytes=64)
+            y_q = work.tile([P, P], U32, name="y_q", align_bytes=64, bufs=4)
+            nc.vector.quantize_mx(out=y_q[:].bitcast(FP8X4), scales=y_s[a][:, P * j:P * (j + 1)], in_=src)
+            nc.sync.dma_start(
+                out=out_1[0, :, P * i:P * (i + 1), :].rearrange("p m t -> p (m t)").bitcast(I32),
+                in_=y_q[:].bitcast(I32),
+            )
+            if j == TILES - 1:
+                for q in range(4):
+                    nc.sync.dma_start(
+                        out=out_2[0, 4 * q:4 * q + 4, T * a:T * (a + 1)].bitcast(I32),
+                        in_=y_s[a][32 * q:32 * q + 4, :].bitcast(I32),
+                    )
+
+        load_dv(0)
+        vref0 = load_vref(0)
+        load_dv(1)
+        load_scales(r_planes[0], r_scales, slice(0, GE))
+        load_r(0, 0)
+        load_dv(2)
+        load_r(0, 1)
+        load_r(0, 2)
+        load_gain(0)
+        load_dv(3)
+        load_c(0)
+        load_rest(0)
+        nc.vector.reciprocal(out=recip[0][:], in_=vref0[:, :, 0:4])
+
+        bank_a, bank_b, mix_a, mix_b = {}, {}, {}, {}
+
+        def turn_hy(key, ih, iy, tag_a, tag_b, bufs):
+            if live(ih):
+                bank_a[key] = psum.tile([P, 4, P], F32, name=tag_a, bufs=bufs)
+                turn_words(bank_a[key], 0, h_bf[ih, 0])
+                turn_words(bank_a[key], 1, h_bf[ih, 1])
+            bank_b[key] = psum.tile([P, 4, P], F32, name=tag_b, bufs=bufs)
+            if live(ih):
+                turn_words(bank_b[key], 0, h_bf[ih, 2])
+            if live(iy):
+                turn_words(bank_b[key], 1, y_bf[iy])
+
+        def copy_hy(key, ih, iy):
+            if live(ih):
+                mix_a[key] = work.tile([P, 2 * KP], BF16, name="mix_a", align_bytes=64)
+                copy_words(mix_a[key], bank_a[key], 0, 2)
+            mix_b[key] = work.tile([P, 2 * KP], BF16, name="mix_b", align_bytes=64, bufs=5)
+            copy_words(mix_b[key], bank_b[key], 0 if live(ih) else 1, 2 if live(iy) else 1)
+
+        def quantize_h(i):
+            h_qa[i] = work.tile([P, 2 * P], U32, name="h_qa", align_bytes=64)
+            h_sa[i] = work.tile([P, 2 * P], U8, name="h_sa", align_bytes=64)
+            nc.vector.quantize_mx(out=h_qa[i][:].bitcast(FP8X4), scales=h_sa[i][:], in_=mix_a[i][:])
+            h_qb[i] = work.tile([P, P], U32, name="h_qb", align_bytes=64)
+            h_sb[i] = work.tile([P, P], U8, name="h_sb", align_bytes=64)
+            nc.vector.quantize_mx(out=h_qb[i][:].bitcast(FP8X4), scales=h_sb[i][:], in_=mix_b[i][:, 0:KP])
+
+        def stiff_on_vector(i):
+            y_own = work.tile([P, N], F32, name="y_own", bufs=3)
+            apply_stiff(i, nc.vector, y_own)
+
+        last = UNITS - 1
+        for s in range(-2, last):
+            if s >= 0 and live(s + 4):
+                load_dv(s + 4)
+            nxt = s // TILES + 1
+            if 0 <= s and nxt < G:
+                if s % TILES == 0:
+                    v = load_vref(nxt)
+                    load_scales(r_planes[nxt], r_scales, slice(GE * nxt, GE * (nxt + 1)))
+                    for c in range(GP):
+                        load_r(nxt, c)
+                if s % TILES == 1:
+                    load_gain(nxt)
+                if s % TILES == 2:
+                    nc.vector.reciprocal(out=recip[nxt][:], in_=v[:, :, 0:4])
+                    load_c(nxt)
+                if s % TILES == 3:
+                    load_rest(nxt)
+
+            ih, iy = s - 2, s - 5
+            if live(ih):
+                turn_hy(ih, ih, iy, "bank_a", "bank_b", 1)
+            if live(s + 2):
+                turn_x(s + 2)
+            if live(s - 4):
+                apply_stiff(s - 4, nc.gpsimd, th[s - 2, GP - 1])
+            if live(s - 3):
+                add_rest(s - 3)
+            if live(s + 1):
+                divide_x(s + 1)
+            if live(ih):
+                copy_hy(ih, ih, iy)
+                quantize_h(ih)
+            if live(iy):
+                quantize_y(iy, mix_b[ih][:, KP:2 * KP])
+            if live(s + 1):
+                quantize_x(s + 1)
+            if live(s):
+                stage1(s)
+            if live(ih):
+                stage2(ih, "z_ps")
+            if live(s):
+                saturate(s)
+            if live(s - 4):
+                round_y(s - 4)
+            if live(s - 1):
+                apply_gain(s - 1)
+
+        turn_hy(13, 13, 10, "bank_a", "bank_b", 1)
+        stage1(15)
+        add_rest(12)
+        stiff_on_vector(11)
+        copy_hy(13, 13, 10)
+        quantize_h(13)
+        quantize_y(10, mix_b[13][:, KP:2 * KP])
+        stage2(13, "z_ps")
+        saturate(15)
+        apply_gain(14)
+        round_y(11)
+        turn_hy(14, 14, 11, "bank_a", "bank_b", 1)
+        apply_gain(15)
+        copy_hy(14, 14, 11)
+        add_rest(13)
+        stiff_on_vector(12)
+        turn_hy(15, 15, -1, "x_ps", "x_ps", 2)
+        quantize_h(14)
+        copy_hy(15, 15, -1)
+        stage2(14, "s_ps0")
+        quantize_h(15)
+        stage2(15, "s_ps1")
+        round_y(12)
+        quantize_y(11, mix_b[14][:, KP:2 * KP])
+        stiff_on_vector(13)
+        turn_hy(16, -1, 12, "bank_a", "bank_b", 1)
+        round_y(13)
+        add_rest(14)
+        copy_hy(16, -1, 12)
+        add_rest(15)
+        turn_hy(17, -1, 13, "bank_a", "bank_a", 1)
+        stiff_on_vector(14)
+        copy_hy(17, -1, 13)
+        round_y(14)
+        stiff_on_vector(15)
+        round_y(15)
+        turn_hy(18, -1, 14, "bank_a", "bank_b", 1)
+        copy_hy(18, -1, 14)
+        turn_hy(19, -1, 15, "bank_a", "bank_a", 1)
+        copy_hy(19, -1, 15)
+        quantize_y(12, mix_b[16][:, KP:2 * KP])
+        quantize_y(13, mix_b[17][:, KP:2 * KP])
+        quantize_y(14, mix_b[18][:, KP:2 * KP])
+        quantize_y(15, mix_b[19][:, KP:2 * KP])

@@ -41,10 +41,10 @@ def tile_tactile_impedance_patches_k7_kernel(
         nc.scalar.activation(out=warm[:, 4:5], in_=warm[:, 0:1], func=ACT.Tanh)
 
         r_planes, c_planes = [], []
-        for a in range(G):
+        for a in range(2):
             r_planes.append(keep.tile([P, GE, PX], U8, name="r_plane%d" % a, align_bytes=64))
             c_planes.append(keep.tile([P, GP, N], U8, name="c_plane%d" % a, align_bytes=64))
-        for a in range(G):
+        for a in range(2):
             nc.vector.memset(r_planes[a][:].rearrange("p g n -> p (g n)").bitcast(I32), 0)
             nc.vector.memset(c_planes[a][:].rearrange("p g n -> p (g n)").bitcast(I32), 0)
 
@@ -81,7 +81,7 @@ def tile_tactile_impedance_patches_k7_kernel(
             nc.sync.dma_start(out=gain_sb[a][:], in_=gain[a].partition_broadcast(P))
 
         def load_c(a):
-            load_scales(c_planes[a], c_scales, slice(GP * a, GP * (a + 1)))
+            load_scales(c_planes[a % 2], c_scales, slice(GP * a, GP * (a + 1)))
             c_sb[a] = keep.tile([P, GP, 2 * N], U8, name="c%d" % a, align_bytes=64)
             nc.sync.dma_start(
                 out=c_sb[a][:].bitcast(I32),
@@ -96,33 +96,39 @@ def tile_tactile_impedance_patches_k7_kernel(
 
         x_ps, x_bf, x_q, x_s, s_ps, th, h_bf = {}, {}, {}, {}, {}, {}, {}
         h_qa, h_sa, h_qb, h_sb, z_ps, y_sb, y_bf, y_s = {}, {}, {}, {}, {}, {}, {}, {}
-        offs = {}
+        offs, h_q, stiff32 = {}, {}, {}
 
         def live(i):
             return 0 <= i < UNITS
 
         def turn_x(i):
-            x_ps[i] = psum.tile([P, 2 * GE, P], F32, name="x_ps", bufs=2)
+            if i == 2:
+                x_ps[i] = psum.tile([P, 2 * GE, P], F32, name="bank_a")
+            else:
+                x_ps[i] = psum.tile([P, 2 * GE, P], F32, name="x_ps", bufs=2)
             words = dv_sb[i][:].bitcast(F32)
             for g in range(GE):
                 for u in range(2):
                     nc.tensor.transpose(x_ps[i][:, 2 * g + u, :], words[:, 256 * g + u:256 * (g + 1):2], ident[:])
 
-        def divide_x(i):
+        def divide_x(i, dst):
             a = i // TILES
-            x_bf[i] = work.tile([P, E], BF16, name="x_bf", align_bytes=64)
             for g in range(GE):
                 nc.vector.tensor_tensor(
-                    out=x_bf[i][:, KP * g:KP * (g + 1)].rearrange("p (r u e) -> p r u e", u=2, e=2),
+                    out=dst[:, KP * g:KP * (g + 1)].rearrange("p (r u e) -> p r u e", u=2, e=2),
                     in0=x_ps[i][:, 2 * g:2 * g + 2, :].bitcast(BF16).rearrange("p u (r e) -> p r u e", e=2),
                     in1=recip[a][:, g, :].rearrange("p (u e) -> p u e", e=2).unsqueeze(1).to_broadcast([P, P, 2, 2]),
                     op=ALU.mult,
                 )
 
-        def quantize_x(i):
-            x_q[i] = work.tile([P, GE * P], U32, name="x_q", align_bytes=64, bufs=3)
-            x_s[i] = work.tile([P, GE * P], U8, name="x_s", align_bytes=64, bufs=3)
-            nc.vector.quantize_mx(out=x_q[i][:].bitcast(FP8X4), scales=x_s[i][:], in_=x_bf[i][:])
+        def quantize(src, tag, lo, hi):
+            width = src.shape[1] // 4
+            codes = work.tile([P, width], U32, name=tag + "_q", align_bytes=64, bufs=3)
+            scales = work.tile([P, width], U8, name=tag + "_s", align_bytes=64, bufs=3)
+            nc.vector.quantize_mx(
+                out=codes[:, P * lo:P * hi].bitcast(FP8X4), scales=scales[:, P * lo:P * hi], in_=src[:, KP * lo:KP * hi]
+            )
+            return [(codes[:, P * k:P * (k + 1)].bitcast(FP8X4), scales[:, P * k:P * (k + 1)]) for k in range(width // P)]
 
         def stage1(i):
             a = i // TILES
@@ -131,42 +137,40 @@ def tile_tactile_impedance_patches_k7_kernel(
                 for g in range(GE):
                     nc.tensor.matmul_mx(
                         out=s_ps[i, c][:],
-                        lhsT=x_q[i][:, P * g:P * (g + 1)].bitcast(FP8X4),
-                        lhsT_scale=x_s[i][:, P * g:P * (g + 1)],
+                        lhsT=x_q[i][g][0],
+                        lhsT_scale=x_q[i][g][1],
                         rhs=r_sb[a, c][:, g, :].bitcast(FP4X4),
-                        rhs_scale=r_planes[a][:, g, KP * c:KP * (c + 1)],
+                        rhs_scale=r_planes[a % 2][:, g, KP * c:KP * (c + 1)],
                         start=(g == 0),
                         stop=(g == GE - 1),
                     )
 
         def saturate(i):
+            th[i] = work.tile([P, 2, GP, KP // 2], F32, name="th")
             for c in range(GP):
-                th[i, c] = work.tile([P, KP], F32, name="th%d" % c, bufs=4 if c == GP - 1 else 2)
                 nc.scalar.activation(
-                    out=th[i, c][:].rearrange("p (u m e) -> p u m e", u=2, e=2),
+                    out=th[i][:, :, c, :].rearrange("p u (m e) -> p u m e", e=2),
                     in_=s_ps[i, c][:].rearrange("p (m u e) -> p u m e", u=2, e=2),
                     func=ACT.Tanh,
                 )
 
         def apply_gain(i):
-            a = i // TILES
-            for c in range(GP):
-                h_bf[i, c] = work.tile([P, KP], BF16, name="h_bf%d" % c)
-                nc.vector.tensor_tensor(
-                    out=h_bf[i, c][:].rearrange("p (u m e) -> p u m e", u=2, e=2),
-                    in0=th[i, c][:].rearrange("p (u m e) -> p u m e", u=2, e=2),
-                    in1=gain_sb[a][:, KP * c:KP * (c + 1)].rearrange("p (m u e) -> p u m e", u=2, e=2),
-                    op=ALU.mult,
-                )
+            h_bf[i] = work.tile([P, PX], BF16, name="h_bf")
+            nc.vector.tensor_tensor(
+                out=h_bf[i][:].rearrange("p (u m e) -> p u m e", u=2, e=2),
+                in0=th[i][:].rearrange("p u c (m e) -> p u (c m) e", e=2),
+                in1=gain_sb[i // TILES][:].rearrange("p (m u e) -> p u m e", u=2, e=2),
+                op=ALU.mult,
+            )
 
-        def turn_words(bank, slot, src):
-            words = src[:].bitcast(F32)
+        def turn_words(bank, slot, src, c):
+            words = src[:].bitcast(F32).rearrange("p (u w) -> p u w", u=2)
             for u in range(2):
-                nc.tensor.transpose(bank[:, 2 * slot + u, :], words[:, P * u:P * (u + 1)], ident[:])
+                nc.tensor.transpose(bank[:, 2 * slot + u, :], words[:, u, P * c:P * (c + 1)], ident[:])
 
         def copy_words(dst, bank, lo, hi):
             nc.scalar.copy(
-                out=dst[:, KP * lo:KP * hi].bitcast(F32).rearrange("p (g r u) -> p g r u", r=P, u=2),
+                out=dst.bitcast(F32).rearrange("p (g r u) -> p g r u", r=P, u=2),
                 in_=bank[:, 2 * lo:2 * hi, :].rearrange("p (g u) r -> p g r u", u=2),
             )
 
@@ -174,13 +178,12 @@ def tile_tactile_impedance_patches_k7_kernel(
             a = i // TILES
             z_ps[i] = psum.tile([P, N], F32, name=tag)
             for g in range(GP):
-                codes, scales, col = (h_qa[i], h_sa[i], g) if g < 2 else (h_qb[i], h_sb[i], 0)
                 nc.tensor.matmul_mx(
                     out=z_ps[i][:],
-                    lhsT=codes[:, P * col:P * (col + 1)].bitcast(FP8X4),
-                    lhsT_scale=scales[:, P * col:P * (col + 1)],
+                    lhsT=h_q[i][g][0],
+                    lhsT_scale=h_q[i][g][1],
                     rhs=c_sb[a][:, g, :].bitcast(FP4X4),
-                    rhs_scale=c_planes[a][:, g, :],
+                    rhs_scale=c_planes[a % 2][:, g, :],
                     start=(g == 0),
                     stop=(g == GP - 1),
                 )
@@ -192,8 +195,8 @@ def tile_tactile_impedance_patches_k7_kernel(
         def apply_stiff(i, eng, dst):
             a, j = divmod(i, TILES)
             y_sb[i] = dst
-            eng.tensor_tensor(out=dst[:], in0=offs[i][:], in1=stiff_sb[a][:], op=ALU.mult)
-            nc.sync.dma_start(out=out_0[a, j * P:(j + 1) * P, :], in_=dst[:])
+            eng.tensor_tensor(out=dst, in0=offs[i][:], in1=stiff32[a][:], op=ALU.mult)
+            nc.sync.dma_start(out=out_0[a, j * P:(j + 1) * P, :], in_=dst)
 
         def stiff_to_words(i):
             y_bf[i] = work.tile([P, N], BF16, name="y_bf", bufs=3)
@@ -208,20 +211,21 @@ def tile_tactile_impedance_patches_k7_kernel(
             y_bf[i] = work.tile([P, N], BF16, name="y_bf", bufs=3)
             nc.scalar.copy(
                 out=y_bf[i][:].rearrange("p (u m e) -> p u m e", u=2, e=2),
-                in_=y_sb[i][:].rearrange("p (m u e) -> p u m e", u=2, e=2),
+                in_=y_sb[i].rearrange("p (m u e) -> p u m e", u=2, e=2),
             )
 
         def quantize_y(i, src):
             a, j = divmod(i, TILES)
+            width = src.shape[1] // 4
             if j == 0:
                 y_s[a] = work.tile([P, T], U8, name="y_s", align_bytes=64)
-            y_q = work.tile([P, P], U32, name="y_q", align_bytes=64, bufs=4)
-            nc.vector.quantize_mx(out=y_q[:].bitcast(FP8X4), scales=y_s[a][:, P * j:P * (j + 1)], in_=src)
+            y_q = work.tile([P, width], U32, name="y_q", align_bytes=64, bufs=4)
+            nc.vector.quantize_mx(out=y_q[:].bitcast(FP8X4), scales=y_s[a][:, P * j:P * j + width], in_=src)
             nc.sync.dma_start(
-                out=out_1[0, :, P * i:P * (i + 1), :].rearrange("p m t -> p (m t)").bitcast(I32),
+                out=out_1[0, :, P * i:P * i + width, :].rearrange("p m t -> p (m t)").bitcast(I32),
                 in_=y_q[:].bitcast(I32),
             )
-            if j == TILES - 1:
+            if P * j + width == T:
                 for q in range(4):
                     nc.sync.dma_start(
                         out=out_2[0, 4 * q:4 * q + 4, T * a:T * (a + 1)].bitcast(I32),
@@ -247,32 +251,40 @@ def tile_tactile_impedance_patches_k7_kernel(
         def turn_hy(key, ih, iy, tag_a, tag_b, bufs):
             if live(ih):
                 bank_a[key] = psum.tile([P, 4, P], F32, name=tag_a, bufs=bufs)
-                turn_words(bank_a[key], 0, h_bf[ih, 0])
-                turn_words(bank_a[key], 1, h_bf[ih, 1])
+                turn_words(bank_a[key], 0, h_bf[ih], 0)
+                turn_words(bank_a[key], 1, h_bf[ih], 1)
             bank_b[key] = psum.tile([P, 4, P], F32, name=tag_b, bufs=bufs)
             if live(ih):
-                turn_words(bank_b[key], 0, h_bf[ih, 2])
+                turn_words(bank_b[key], 0, h_bf[ih], 2)
             if live(iy):
-                turn_words(bank_b[key], 1, y_bf[iy])
+                turn_words(bank_b[key], 1, y_bf[iy], 0)
+
+        def new_mix_a(key):
+            mix_a[key] = work.tile([P, 4 * KP], BF16, name="mix_a", align_bytes=64, bufs=3)
 
         def copy_hy(key, ih, iy):
             if live(ih):
-                mix_a[key] = work.tile([P, 2 * KP], BF16, name="mix_a", align_bytes=64)
-                copy_words(mix_a[key], bank_a[key], 0, 2)
+                copy_words(mix_a[key][:, 2 * KP:4 * KP], bank_a[key], 0, 2)
             mix_b[key] = work.tile([P, 2 * KP], BF16, name="mix_b", align_bytes=64, bufs=5)
-            copy_words(mix_b[key], bank_b[key], 0 if live(ih) else 1, 2 if live(iy) else 1)
+            lo, hi = (0 if live(ih) else 1), (2 if live(iy) else 1)
+            copy_words(mix_b[key][:, KP * lo:KP * hi], bank_b[key], lo, hi)
 
-        def quantize_h(i):
-            h_qa[i] = work.tile([P, 2 * P], U32, name="h_qa", align_bytes=64)
-            h_sa[i] = work.tile([P, 2 * P], U8, name="h_sa", align_bytes=64)
-            nc.vector.quantize_mx(out=h_qa[i][:].bitcast(FP8X4), scales=h_sa[i][:], in_=mix_a[i][:])
-            h_qb[i] = work.tile([P, P], U32, name="h_qb", align_bytes=64)
-            h_sb[i] = work.tile([P, P], U8, name="h_sb", align_bytes=64)
-            nc.vector.quantize_mx(out=h_qb[i][:].bitcast(FP8X4), scales=h_sb[i][:], in_=mix_b[i][:, 0:KP])
+        def quantize_xh(key, ix, ih):
+            ops = quantize(mix_a[key], "a", 0 if live(ix) else 2, 4 if live(ih) else 2)
+            x_q[ix] = ops[0:2]
+            if live(ih):
+                h_q[ih] = ops[2:4] + quantize(mix_b[key][:, 0:KP], "b", 0, 1)
+
+        def turn_y_run(key, tiles, tag):
+            bank_b[key] = psum.tile([P, 4, P], F32, name=tag)
+            for slot, i in enumerate(tiles):
+                turn_words(bank_b[key], slot, y_bf[i], 0)
+            mix_b[key] = work.tile([P, 2 * KP], BF16, name="mix_b", align_bytes=64, bufs=5)
+            copy_words(mix_b[key][:, 0:KP * len(tiles)], bank_b[key], 0, len(tiles))
 
         def stiff_on_vector(i):
             y_own = work.tile([P, N], F32, name="y_own", bufs=3)
-            apply_stiff(i, nc.vector, y_own)
+            apply_stiff(i, nc.vector, y_own[:])
 
         last = UNITS - 1
         for s in range(-2, last):
@@ -282,7 +294,7 @@ def tile_tactile_impedance_patches_k7_kernel(
             if 0 <= s and nxt < G:
                 if s % TILES == 0:
                     v = load_vref(nxt)
-                    load_scales(r_planes[nxt], r_scales, slice(GE * nxt, GE * (nxt + 1)))
+                    load_scales(r_planes[nxt % 2], r_scales, slice(GE * nxt, GE * (nxt + 1)))
                     for c in range(GP):
                         load_r(nxt, c)
                 if s % TILES == 1:
@@ -293,76 +305,78 @@ def tile_tactile_impedance_patches_k7_kernel(
                 if s % TILES == 3:
                     load_rest(nxt)
 
-            ih, iy = s - 2, s - 5
+            ix, ih, iy = s + 1, s - 2, s - 5
             if live(ih):
-                turn_hy(ih, ih, iy, "bank_a", "bank_b", 1)
+                turn_hy(s, ih, iy, "bank_a", "bank_b", 1)
             if live(s + 2):
                 turn_x(s + 2)
             if live(s - 4):
-                apply_stiff(s - 4, nc.gpsimd, th[s - 2, GP - 1])
+                apply_stiff(s - 4, nc.gpsimd, mix_b[s - 1][:].bitcast(F32))
+            if live(ix):
+                new_mix_a(s)
+                divide_x(ix, mix_a[s])
             if live(s - 3):
                 add_rest(s - 3)
-            if live(s + 1):
-                divide_x(s + 1)
             if live(ih):
-                copy_hy(ih, ih, iy)
-                quantize_h(ih)
-            if live(iy):
-                quantize_y(iy, mix_b[ih][:, KP:2 * KP])
-            if live(s + 1):
-                quantize_x(s + 1)
+                copy_hy(s, ih, iy)
+            if s % TILES == 2 and live(s):
+                stiff32[s // TILES] = work.tile([P, N], F32, name="stiff32")
+                nc.scalar.copy(out=stiff32[s // TILES][:], in_=stiff_sb[s // TILES][:])
+            if live(s - 4):
+                round_y(s - 4)
             if live(s):
                 stage1(s)
+            if live(ix) and not live(ih):
+                quantize_xh(s, ix, ih)
+            if live(s - 1):
+                apply_gain(s - 1)
+            if live(ih):
+                quantize_xh(s, ix, ih)
+            if live(iy):
+                quantize_y(iy, mix_b[s][:, KP:2 * KP])
             if live(ih):
                 stage2(ih, "z_ps")
             if live(s):
                 saturate(s)
-            if live(s - 4):
-                round_y(s - 4)
-            if live(s - 1):
-                apply_gain(s - 1)
 
-        turn_hy(13, 13, 10, "bank_a", "bank_b", 1)
-        stage1(15)
-        add_rest(12)
         stiff_on_vector(11)
-        copy_hy(13, 13, 10)
-        quantize_h(13)
-        quantize_y(10, mix_b[13][:, KP:2 * KP])
-        stage2(13, "z_ps")
-        saturate(15)
+        turn_hy(15, 13, 10, "bank_a", "bank_b", 1)
+        stage1(15)
         apply_gain(14)
-        round_y(11)
-        turn_hy(14, 14, 11, "bank_a", "bank_b", 1)
-        apply_gain(15)
-        copy_hy(14, 14, 11)
-        add_rest(13)
+        new_mix_a(15)
+        copy_hy(15, 13, 10)
+        add_rest(12)
+        quantize_xh(15, -1, 13)
+        quantize_y(10, mix_b[15][:, KP:2 * KP])
+        saturate(15)
+        turn_hy(16, 14, -1, "x_ps", "x_ps", 2)
+        stage2(13, "z_ps")
         stiff_on_vector(12)
-        turn_hy(15, 15, -1, "x_ps", "x_ps", 2)
-        quantize_h(14)
-        copy_hy(15, 15, -1)
-        stage2(14, "s_ps0")
-        quantize_h(15)
-        stage2(15, "s_ps1")
+        new_mix_a(16)
+        copy_hy(16, 14, -1)
+        apply_gain(15)
+        round_y(11)
         round_y(12)
-        quantize_y(11, mix_b[14][:, KP:2 * KP])
+        quantize_xh(16, -1, 14)
+        turn_hy(17, 15, 11, "bank_a", "bank_b", 1)
+        stage2(14, "s_ps0")
+        add_rest(13)
+        new_mix_a(17)
+        copy_hy(17, 15, 11)
         stiff_on_vector(13)
-        turn_hy(16, -1, 12, "bank_a", "bank_b", 1)
+        quantize_xh(17, -1, 15)
+        stage2(15, "s_ps1")
         round_y(13)
         add_rest(14)
-        copy_hy(16, -1, 12)
-        add_rest(15)
-        turn_hy(17, -1, 13, "bank_a", "bank_a", 1)
+        quantize_y(11, mix_b[17][:, KP:2 * KP])
+        turn_y_run(18, [12, 13], "bank_a")
         stiff_on_vector(14)
-        copy_hy(17, -1, 13)
+        add_rest(15)
         round_y(14)
+        stiff_to_words(15)
+        quantize_y(12, mix_b[18][:])
+        turn_y_run(19, [14], "bank_b")
+        turn_y_run(20, [15], "s_ps2")
         stiff_on_vector(15)
-        round_y(15)
-        turn_hy(18, -1, 14, "bank_a", "bank_b", 1)
-        copy_hy(18, -1, 14)
-        turn_hy(19, -1, 15, "bank_a", "bank_a", 1)
-        copy_hy(19, -1, 15)
-        quantize_y(12, mix_b[16][:, KP:2 * KP])
-        quantize_y(13, mix_b[17][:, KP:2 * KP])
-        quantize_y(14, mix_b[18][:, KP:2 * KP])
-        quantize_y(15, mix_b[19][:, KP:2 * KP])
+        quantize_y(14, mix_b[19][:, 0:KP])
+        quantize_y(15, mix_b[20][:, 0:KP])

@@ -22,6 +22,8 @@ GE = E // KP
 GP = PX // KP
 TILES = T // P
 UNITS = G * TILES
+SHARE = 640
+AHEAD = 4
 
 
 def tile_tactile_impedance_patches_k7_kernel(
@@ -48,19 +50,20 @@ def tile_tactile_impedance_patches_k7_kernel(
             nc.vector.memset(r_planes[a][:].rearrange("p g n -> p (g n)").bitcast(I32), 0)
             nc.vector.memset(c_planes[a][:].rearrange("p g n -> p (g n)").bitcast(I32), 0)
 
-        dv_sb, r_sb, c_sb, gain_sb, rest_sb, stiff_sb, recip = {}, {}, {}, {}, {}, {}, {}
+        dv_sb, r_sb, c_sb, gain_sb, rest_sb, stiff_sb = {}, {}, {}, {}, {}, {}
 
         def load_dv(i):
             a, j = divmod(i, TILES)
-            dv_sb[i] = work.tile([P, E], BF16, name="dv_t", bufs=5)
+            dv_sb[i] = work.tile([P, E], BF16, name="dv_t", bufs=6)
             nc.sync.dma_start(out=dv_sb[i][:], in_=dv[a, j * P:(j + 1) * P, :])
 
-        def load_vref(a):
-            v = keep.tile([P, GE, 16], BF16, name="vref%d" % a)
+        def load_vref(lo, hi):
+            rows = keep.tile([P, GE * (hi - lo), 16], BF16, name="vref%d" % lo)
             with nc.allow_non_contiguous_dma("four values a partition and group"):
-                nc.sync.dma_start(out=v[:, :, 0:4], in_=vref[a].rearrange("(g p t) -> p g t", g=GE, t=4))
-            recip[a] = keep.tile([P, GE, 4], F32, name="recip%d" % a)
-            return v
+                nc.sync.dma_start(out=rows[:, :, 0:4], in_=vref[lo:hi].rearrange("a (g p t) -> p (a g) t", g=GE, t=4))
+            return rows
+
+        recip = keep.tile([P, G * GE, 4], F32, name="recip")
 
         def load_scales(plane, scales, groups):
             for q in range(4):
@@ -69,16 +72,21 @@ def tile_tactile_impedance_patches_k7_kernel(
                     in_=scales[groups, 4 * q:4 * q + 4, :].rearrange("g r n -> r g n").bitcast(I32),
                 )
 
-        def load_r(a, c):
-            r_sb[a, c] = keep.tile([P, GE, 2 * KP], U8, name="r%d_%d" % (a, c), align_bytes=64)
-            nc.sync.dma_start(
-                out=r_sb[a, c][:].bitcast(I32),
-                in_=r_words[GE * a:GE * (a + 1), :, 2 * KP * c:2 * KP * (c + 1)].rearrange("g p n -> p g n").bitcast(I32),
-            )
+        def load_r(a, g):
+            r_sb[a, g] = work.tile([P, 2 * PX], U8, name="r_words%d" % g, align_bytes=64)
+            nc.sync.dma_start(out=r_sb[a, g][:].bitcast(I32), in_=r_words[GE * a + g].bitcast(I32))
 
         def load_gain(a):
-            gain_sb[a] = keep.tile([P, PX], BF16, name="gain%d" % a)
+            gain_sb[a] = work.tile([P, PX], BF16, name="gain_row")
             nc.sync.dma_start(out=gain_sb[a][:], in_=gain[a].partition_broadcast(P))
+
+        def sort_gain(a, lo, hi, copy):
+            if lo == 0:
+                gain32[a] = work.tile([P, PX], F32, name="gain32")
+            copy(
+                out=gain32[a][:, KP * lo:KP * hi].rearrange("p (c u m e) -> p c u m e", c=hi - lo, u=2, e=2),
+                in_=gain_sb[a][:, KP * lo:KP * hi].rearrange("p (c m u e) -> p c u m e", c=hi - lo, u=2, e=2),
+            )
 
         def load_c(a):
             load_scales(c_planes[a % 2], c_scales, slice(GP * a, GP * (a + 1)))
@@ -96,77 +104,83 @@ def tile_tactile_impedance_patches_k7_kernel(
 
         x_ps, x_bf, x_q, x_s, s_ps, th, h_bf = {}, {}, {}, {}, {}, {}, {}
         h_qa, h_sa, h_qb, h_sb, z_ps, y_sb, y_bf, y_s = {}, {}, {}, {}, {}, {}, {}, {}
-        offs, h_q, stiff32 = {}, {}, {}
+        offs, h_q, gain32 = {}, {}, {}
 
         def live(i):
             return 0 <= i < UNITS
 
-        def turn_x(i):
-            if i == 2:
-                x_ps[i] = psum.tile([P, 2 * GE, P], F32, name="bank_a")
-            else:
-                x_ps[i] = psum.tile([P, 2 * GE, P], F32, name="x_ps", bufs=2)
+        def turn_x(i, tag, bufs):
+            x_ps[i] = psum.tile([P, GE, 2 * P], F32, name=tag, bufs=bufs)
             words = dv_sb[i][:].bitcast(F32)
             for g in range(GE):
                 for u in range(2):
-                    nc.tensor.transpose(x_ps[i][:, 2 * g + u, :], words[:, 256 * g + u:256 * (g + 1):2], ident[:])
+                    nc.tensor.transpose(x_ps[i][:, g, u:2 * P:2], words[:, 256 * g + u:256 * (g + 1):2], ident[:])
 
         def divide_x(i, dst):
             a = i // TILES
-            for g in range(GE):
-                nc.vector.tensor_tensor(
-                    out=dst[:, KP * g:KP * (g + 1)].rearrange("p (r u e) -> p r u e", u=2, e=2),
-                    in0=x_ps[i][:, 2 * g:2 * g + 2, :].bitcast(BF16).rearrange("p u (r e) -> p r u e", e=2),
-                    in1=recip[a][:, g, :].rearrange("p (u e) -> p u e", e=2).unsqueeze(1).to_broadcast([P, P, 2, 2]),
-                    op=ALU.mult,
-                )
+            nc.vector.tensor_tensor(
+                out=dst[:, 0:E].rearrange("p (g r t) -> p g r t", r=P, t=4),
+                in0=x_ps[i][:].bitcast(BF16).rearrange("p g (r t) -> p g r t", t=4),
+                in1=recip[:, GE * a:GE * (a + 1), :].unsqueeze(2).to_broadcast([P, GE, P, 4]),
+                op=ALU.mult,
+            )
 
         def quantize(src, tag, lo, hi):
             width = src.shape[1] // 4
-            codes = work.tile([P, width], U32, name=tag + "_q", align_bytes=64, bufs=3)
-            scales = work.tile([P, width], U8, name=tag + "_s", align_bytes=64, bufs=3)
+            codes = work.tile([P, width], U32, name=tag + "_q", align_bytes=64, bufs=4)
+            scales = work.tile([P, width], U8, name=tag + "_s", align_bytes=64, bufs=4)
             nc.vector.quantize_mx(
                 out=codes[:, P * lo:P * hi].bitcast(FP8X4), scales=scales[:, P * lo:P * hi], in_=src[:, KP * lo:KP * hi]
             )
             return [(codes[:, P * k:P * (k + 1)].bitcast(FP8X4), scales[:, P * k:P * (k + 1)]) for k in range(width // P)]
 
-        def stage1(i):
+        def stage1_pass(i, c, g):
             a = i // TILES
-            for c in range(GP):
+            if g == 0:
                 s_ps[i, c] = psum.tile([P, KP], F32, name="s_ps%d" % c)
+            nc.tensor.matmul_mx(
+                out=s_ps[i, c][:],
+                lhsT=x_q[i][g][0],
+                lhsT_scale=x_q[i][g][1],
+                rhs=r_sb[a, g][:, 2 * KP * c:2 * KP * (c + 1)].bitcast(FP4X4),
+                rhs_scale=r_planes[a % 2][:, g, KP * c:KP * (c + 1)],
+                start=(g == 0),
+                stop=(g == GE - 1),
+            )
+
+        def stage1(i):
+            for c in range(GP):
                 for g in range(GE):
-                    nc.tensor.matmul_mx(
-                        out=s_ps[i, c][:],
-                        lhsT=x_q[i][g][0],
-                        lhsT_scale=x_q[i][g][1],
-                        rhs=r_sb[a, c][:, g, :].bitcast(FP4X4),
-                        rhs_scale=r_planes[a % 2][:, g, KP * c:KP * (c + 1)],
-                        start=(g == 0),
-                        stop=(g == GE - 1),
-                    )
+                    stage1_pass(i, c, g)
 
         def saturate(i):
-            th[i] = work.tile([P, 2, GP, KP // 2], F32, name="th")
+            th[i] = work.tile([P, PX], F32, name="th")
             for c in range(GP):
                 nc.scalar.activation(
-                    out=th[i][:, :, c, :].rearrange("p u (m e) -> p u m e", e=2),
+                    out=th[i][:, KP * c:KP * (c + 1)].rearrange("p (u m e) -> p u m e", u=2, e=2),
                     in_=s_ps[i, c][:].rearrange("p (m u e) -> p u m e", u=2, e=2),
                     func=ACT.Tanh,
                 )
 
-        def apply_gain(i):
-            h_bf[i] = work.tile([P, PX], BF16, name="h_bf")
-            nc.vector.tensor_tensor(
-                out=h_bf[i][:].rearrange("p (u m e) -> p u m e", u=2, e=2),
-                in0=th[i][:].rearrange("p u c (m e) -> p u (c m) e", e=2),
-                in1=gain_sb[i // TILES][:].rearrange("p (m u e) -> p u m e", u=2, e=2),
-                op=ALU.mult,
+        def apply_gain(eng, i, lo, hi):
+            eng.tensor_tensor(
+                out=h_bf[i][:, lo:hi], in0=th[i][:, lo:hi], in1=gain32[i // TILES][:, lo:hi], op=ALU.mult
             )
 
+        def apply_gain_by_group(i):
+            for c in range(GP):
+                cols = slice(KP * c, KP * (c + 1))
+                nc.vector.tensor_tensor(
+                    out=h_bf[i][:, cols].rearrange("p (u m e) -> p u m e", u=2, e=2),
+                    in0=th[i][:, cols].rearrange("p (u m e) -> p u m e", u=2, e=2),
+                    in1=gain_sb[i // TILES][:, cols].rearrange("p (m u e) -> p u m e", u=2, e=2),
+                    op=ALU.mult,
+                )
+
         def turn_words(bank, slot, src, c):
-            words = src[:].bitcast(F32).rearrange("p (u w) -> p u w", u=2)
+            words = src[:, KP * c:KP * (c + 1)].bitcast(F32)
             for u in range(2):
-                nc.tensor.transpose(bank[:, 2 * slot + u, :], words[:, u, P * c:P * (c + 1)], ident[:])
+                nc.tensor.transpose(bank[:, 2 * slot + u, :], words[:, P * u:P * (u + 1)], ident[:])
 
         def copy_words(dst, bank, lo, hi):
             nc.scalar.copy(
@@ -195,7 +209,7 @@ def tile_tactile_impedance_patches_k7_kernel(
         def apply_stiff(i, eng, dst):
             a, j = divmod(i, TILES)
             y_sb[i] = dst
-            eng.tensor_tensor(out=dst, in0=offs[i][:], in1=stiff32[a][:], op=ALU.mult)
+            eng.tensor_tensor(out=dst, in0=offs[i][:], in1=stiff_sb[a][:], op=ALU.mult)
             nc.sync.dma_start(out=out_0[a, j * P:(j + 1) * P, :], in_=dst)
 
         def stiff_to_words(i):
@@ -227,26 +241,26 @@ def tile_tactile_impedance_patches_k7_kernel(
             )
             if P * j + width == T:
                 for q in range(4):
-                    nc.sync.dma_start(
+                    queue = nc.scalar if a == G - 1 and q % 2 == 1 else nc.sync
+                    queue.dma_start(
                         out=out_2[0, 4 * q:4 * q + 4, T * a:T * (a + 1)].bitcast(I32),
                         in_=y_s[a][32 * q:32 * q + 4, :].bitcast(I32),
                     )
 
         load_dv(0)
-        vref0 = load_vref(0)
-        load_dv(1)
+        vref0 = load_vref(0, 1)
+        for i in range(1, AHEAD):
+            load_dv(i)
         load_scales(r_planes[0], r_scales, slice(0, GE))
-        load_r(0, 0)
-        load_dv(2)
-        load_r(0, 1)
-        load_r(0, 2)
+        for g in range(GE):
+            load_r(0, g)
         load_gain(0)
-        load_dv(3)
+        vref_rest = load_vref(1, G)
         load_c(0)
         load_rest(0)
-        nc.vector.reciprocal(out=recip[0][:], in_=vref0[:, :, 0:4])
+        nc.vector.reciprocal(out=recip[:, 0:GE, :], in_=vref0[:, :, 0:4])
 
-        bank_a, bank_b, mix_a, mix_b = {}, {}, {}, {}
+        bank_a, bank_b, mix, third, y_in = {}, {}, {}, {}, {}
 
         def turn_hy(key, ih, iy, tag_a, tag_b, bufs):
             if live(ih):
@@ -259,124 +273,146 @@ def tile_tactile_impedance_patches_k7_kernel(
             if live(iy):
                 turn_words(bank_b[key], 1, y_bf[iy], 0)
 
-        def new_mix_a(key):
-            mix_a[key] = work.tile([P, 4 * KP], BF16, name="mix_a", align_bytes=64, bufs=3)
+        def new_mix(key):
+            mix[key] = work.tile([P, 4 * KP], BF16, name="mix", align_bytes=64, bufs=4)
+
+        def new_third():
+            fresh = work.tile([P, PX], BF16, name="third", align_bytes=64, bufs=4)
+            return fresh
+
+        def copy_y(i, bank, lo, hi):
+            if i % 2 == 0:
+                y_in[i // 2] = work.tile([P, 2 * KP], BF16, name="y_in", align_bytes=64)
+            copy_words(y_in[i // 2][:, KP * (i % 2):KP * (i % 2 + hi - lo)], bank, lo, hi)
 
         def copy_hy(key, ih, iy):
-            if live(ih):
-                copy_words(mix_a[key][:, 2 * KP:4 * KP], bank_a[key], 0, 2)
-            mix_b[key] = work.tile([P, 2 * KP], BF16, name="mix_b", align_bytes=64, bufs=5)
-            lo, hi = (0 if live(ih) else 1), (2 if live(iy) else 1)
-            copy_words(mix_b[key][:, KP * lo:KP * hi], bank_b[key], lo, hi)
+            copy_words(mix[key][:, 2 * KP:4 * KP], bank_a[key], 0, 2)
+            third[key] = new_third()
+            copy_words(third[key][:, 0:KP], bank_b[key], 0, 1)
+            if live(iy):
+                copy_y(iy, bank_b[key], 1, 2)
 
-        def quantize_xh(key, ix, ih):
-            ops = quantize(mix_a[key], "a", 0 if live(ix) else 2, 4 if live(ih) else 2)
-            x_q[ix] = ops[0:2]
-            if live(ih):
-                h_q[ih] = ops[2:4] + quantize(mix_b[key][:, 0:KP], "b", 0, 1)
+        def quantize_mix(key, ix, ih):
+            ops = quantize(mix[key], "a", 0 if live(ix) else 2, 4 if live(ih) else 2)
+            x_q[ix], h_q[ih] = ops[0:2], ops[2:4]
 
-        def turn_y_run(key, tiles, tag):
-            bank_b[key] = psum.tile([P, 4, P], F32, name=tag)
-            for slot, i in enumerate(tiles):
-                turn_words(bank_b[key], slot, y_bf[i], 0)
-            mix_b[key] = work.tile([P, 2 * KP], BF16, name="mix_b", align_bytes=64, bufs=5)
-            copy_words(mix_b[key][:, 0:KP * len(tiles)], bank_b[key], 0, len(tiles))
+        def quantize_third(key, ih):
+            h_q[ih] = h_q[ih] + quantize(third[key][:, 0:KP], "b", 0, 1)
+
+        def turn_y_pair(i, tag):
+            bank = psum.tile([P, 4, P], F32, name=tag)
+            turn_words(bank, 0, y_bf[i], 0)
+            turn_words(bank, 1, y_bf[i + 1], 0)
+            copy_y(i, bank, 0, 2)
 
         def stiff_on_vector(i):
-            y_own = work.tile([P, N], F32, name="y_own", bufs=3)
+            y_own = work.tile([P, N], F32, name="y_own", bufs=4)
             apply_stiff(i, nc.vector, y_own[:])
 
         last = UNITS - 1
-        for s in range(-2, last):
-            if s >= 0 and live(s + 4):
+        for i in range(AHEAD):
+            turn_x(i, *[("x_ps", 2), ("x_ps", 2), ("bank_a", 1), ("bank_b", 1)][i])
+            new_mix(i - 1)
+            divide_x(i, mix[i - 1])
+            if i > 0:
+                quantize_mix(i - 2, i - 1, -1)
+        for s in range(0, last):
+            if live(s + 4):
                 load_dv(s + 4)
             nxt = s // TILES + 1
-            if 0 <= s and nxt < G:
-                if s % TILES == 0:
-                    v = load_vref(nxt)
-                    load_scales(r_planes[nxt % 2], r_scales, slice(GE * nxt, GE * (nxt + 1)))
-                    for c in range(GP):
-                        load_r(nxt, c)
-                if s % TILES == 1:
-                    load_gain(nxt)
-                if s % TILES == 2:
-                    nc.vector.reciprocal(out=recip[nxt][:], in_=v[:, :, 0:4])
-                    load_c(nxt)
-                if s % TILES == 3:
-                    load_rest(nxt)
+            if nxt < G and s % TILES == 1:
+                load_scales(r_planes[nxt % 2], r_scales, slice(GE * nxt, GE * (nxt + 1)))
+                for g in range(GE):
+                    load_r(nxt, g)
+            if nxt < G and s % TILES == 0:
+                load_gain(nxt)
+            if nxt < G and s % TILES == 3:
+                load_c(nxt)
+            if s > 0 and s % TILES == 0:
+                load_rest(s // TILES)
+            if s == 2:
+                nc.vector.reciprocal(out=recip[:, GE:, :], in_=vref_rest[:, :, 0:4])
 
-            ix, ih, iy = s + 1, s - 2, s - 5
+            ix, ig, ih, iz, iy = s + 1, s - 1, s - 2, s - 3, s - 4
+            shared = s - 1 in third
             if live(ih):
-                turn_hy(s, ih, iy, "bank_a", "bank_b", 1)
-            if live(s + 2):
-                turn_x(s + 2)
-            if live(s - 4):
-                apply_stiff(s - 4, nc.gpsimd, mix_b[s - 1][:].bitcast(F32))
-            if live(ix):
-                new_mix_a(s)
-                divide_x(ix, mix_a[s])
-            if live(s - 3):
-                add_rest(s - 3)
+                turn_hy(s, ih, -1, "bank_a", "bank_b", 1)
+            if AHEAD <= s + 2 < UNITS:
+                turn_x(s + 2, "x_ps", 2)
+            if live(iy):
+                turn_words(bank_b[s], 1, y_bf[iy], 0)
+            if live(ig):
+                h_bf[ig] = third[s - 1] if shared else new_third()
+            if shared:
+                apply_gain(nc.gpsimd, ig, 0, SHARE)
+            if ix >= AHEAD:
+                new_mix(s)
+                divide_x(ix, mix[s])
+            if live(iz):
+                add_rest(iz)
             if live(ih):
                 copy_hy(s, ih, iy)
-            if s % TILES == 2 and live(s):
-                stiff32[s // TILES] = work.tile([P, N], F32, name="stiff32")
-                nc.scalar.copy(out=stiff32[s // TILES][:], in_=stiff_sb[s // TILES][:])
-            if live(s - 4):
-                round_y(s - 4)
-            if live(s):
-                stage1(s)
-            if live(ix) and not live(ih):
-                quantize_xh(s, ix, ih)
-            if live(s - 1):
-                apply_gain(s - 1)
+            stage1(s)
+            if shared:
+                apply_gain(nc.vector, ig, SHARE, PX)
+            elif live(ig):
+                apply_gain_by_group(ig)
+            if s == 2:
+                sort_gain(0, 0, GP, nc.vector.tensor_copy)
+            if live(iz):
+                stiff_on_vector(iz)
             if live(ih):
-                quantize_xh(s, ix, ih)
-            if live(iy):
-                quantize_y(iy, mix_b[s][:, KP:2 * KP])
+                quantize_mix(s, ix, ih)
+            if live(iy) and iy % 2 == 1:
+                quantize_y(iy - 1, y_in[iy // 2][:])
             if live(ih):
+                quantize_third(s, ih)
                 stage2(ih, "z_ps")
             if live(s):
                 saturate(s)
+            if live(iz):
+                round_y(iz)
+            if s % TILES > 0 and nxt < G and s > 1:
+                sort_gain(nxt, 0 if s == 2 else s % TILES - 1, s % TILES, nc.scalar.copy)
 
-        stiff_on_vector(11)
-        turn_hy(15, 13, 10, "bank_a", "bank_b", 1)
+        turn_hy(15, 13, 11, "bank_a", "bank_b", 1)
         stage1(15)
-        apply_gain(14)
-        new_mix_a(15)
-        copy_hy(15, 13, 10)
+        h_bf[14] = new_third()
+        apply_gain(nc.vector, 14, 0, PX)
+        new_mix(15)
+        copy_hy(15, 13, 11)
         add_rest(12)
-        quantize_xh(15, -1, 13)
-        quantize_y(10, mix_b[15][:, KP:2 * KP])
+        quantize_mix(15, -1, 13)
+        quantize_third(15, 13)
         saturate(15)
         turn_hy(16, 14, -1, "x_ps", "x_ps", 2)
         stage2(13, "z_ps")
         stiff_on_vector(12)
-        new_mix_a(16)
+        quantize_y(10, y_in[5][:])
+        new_mix(16)
         copy_hy(16, 14, -1)
-        apply_gain(15)
-        round_y(11)
+        h_bf[15] = new_third()
+        apply_gain_by_group(15)
         round_y(12)
-        quantize_xh(16, -1, 14)
-        turn_hy(17, 15, 11, "bank_a", "bank_b", 1)
-        stage2(14, "s_ps0")
         add_rest(13)
-        new_mix_a(17)
-        copy_hy(17, 15, 11)
+        quantize_mix(16, -1, 14)
+        quantize_third(16, 14)
+        turn_hy(17, 15, -1, "bank_a", "bank_b", 1)
+        stage2(14, "s_ps0")
+        new_mix(17)
+        copy_hy(17, 15, -1)
         stiff_on_vector(13)
-        quantize_xh(17, -1, 15)
-        stage2(15, "s_ps1")
         round_y(13)
+        quantize_mix(17, -1, 15)
+        quantize_third(17, 15)
+        stage2(15, "s_ps1")
+        turn_y_pair(12, "bank_a")
         add_rest(14)
-        quantize_y(11, mix_b[17][:, KP:2 * KP])
-        turn_y_run(18, [12, 13], "bank_a")
-        stiff_on_vector(14)
         add_rest(15)
+        stiff_on_vector(14)
         round_y(14)
         stiff_to_words(15)
-        quantize_y(12, mix_b[18][:])
-        turn_y_run(19, [14], "bank_b")
-        turn_y_run(20, [15], "s_ps2")
+        quantize_y(12, y_in[6][:])
+        turn_y_pair(14, "bank_b")
         stiff_on_vector(15)
-        quantize_y(14, mix_b[19][:, 0:KP])
-        quantize_y(15, mix_b[20][:, 0:KP])
+        quantize_y(14, y_in[7][:])

@@ -22,7 +22,6 @@ GE = E // KP
 GP = PX // KP
 TILES = T // P
 UNITS = G * TILES
-SHARE = 640
 AHEAD = 4
 
 
@@ -50,7 +49,18 @@ def tile_tactile_impedance_patches_k7_kernel(
             nc.vector.memset(r_planes[a][:].rearrange("p g n -> p (g n)").bitcast(I32), 0)
             nc.vector.memset(c_planes[a][:].rearrange("p g n -> p (g n)").bitcast(I32), 0)
 
-        dv_sb, r_sb, c_sb, gain_sb, rest_sb, stiff_sb = {}, {}, {}, {}, {}, {}
+        def by_words(ap):
+            return ap.rearrange("p (u m e) -> p u m e", u=2, e=2)
+
+        def pick_words(ap):
+            return ap.rearrange("p (m u e) -> p u m e", u=2, e=2)
+
+        def group(ap, c):
+            if c == 0:
+                return by_words(ap[:, 0:KP])
+            return by_words(ap[:, KP:PX])[:, :, P * (c - 1):P * c, :]
+
+        dv_sb, r_sb, c_sb = {}, {}, {}
 
         def load_dv(i):
             a, j = divmod(i, TILES)
@@ -76,17 +86,15 @@ def tile_tactile_impedance_patches_k7_kernel(
             r_sb[a, g] = work.tile([P, 2 * PX], U8, name="r_words%d" % g, align_bytes=64)
             nc.sync.dma_start(out=r_sb[a, g][:].bitcast(I32), in_=r_words[GE * a + g].bitcast(I32))
 
-        def load_gain(a):
-            gain_sb[a] = work.tile([P, PX], BF16, name="gain_row")
-            nc.sync.dma_start(out=gain_sb[a][:], in_=gain[a].partition_broadcast(P))
+        def load_rows(name, vector, lo, hi):
+            width = vector.shape[1]
+            rows = keep.tile([P, (hi - lo) * width], BF16, name=name)
+            nc.sync.dma_start(out=rows[:], in_=vector[lo:hi].rearrange("a n -> (a n)").partition_broadcast(P))
+            return {a: rows[:, width * (a - lo):width * (a - lo + 1)] for a in range(lo, hi)}
 
-        def sort_gain(a, lo, hi, copy):
-            if lo == 0:
-                gain32[a] = work.tile([P, PX], F32, name="gain32")
-            copy(
-                out=gain32[a][:, KP * lo:KP * hi].rearrange("p (c u m e) -> p c u m e", c=hi - lo, u=2, e=2),
-                in_=gain_sb[a][:, KP * lo:KP * hi].rearrange("p (c m u e) -> p c u m e", c=hi - lo, u=2, e=2),
-            )
+        def sort_gain(a, copy):
+            gain32[a] = work.tile([P, KP], F32, name="gain32")
+            copy(out=by_words(gain32[a][:]), in_=pick_words(gain_sb[a][:, 0:KP]))
 
         def load_c(a):
             load_scales(c_planes[a % 2], c_scales, slice(GP * a, GP * (a + 1)))
@@ -96,12 +104,6 @@ def tile_tactile_impedance_patches_k7_kernel(
                 in_=c_words[GP * a:GP * (a + 1)].rearrange("g p n -> p g n").bitcast(I32),
             )
 
-        def load_rest(a):
-            rest_sb[a] = keep.tile([P, N], BF16, name="rest%d" % a)
-            nc.sync.dma_start(out=rest_sb[a][:], in_=rest[a].partition_broadcast(P))
-            stiff_sb[a] = keep.tile([P, N], BF16, name="stiff%d" % a)
-            nc.sync.dma_start(out=stiff_sb[a][:], in_=stiff[a].partition_broadcast(P))
-
         x_ps, x_bf, x_q, x_s, s_ps, th, h_bf = {}, {}, {}, {}, {}, {}, {}
         h_qa, h_sa, h_qb, h_sb, z_ps, y_sb, y_bf, y_s = {}, {}, {}, {}, {}, {}, {}, {}
         offs, h_q, gain32 = {}, {}, {}
@@ -110,20 +112,21 @@ def tile_tactile_impedance_patches_k7_kernel(
             return 0 <= i < UNITS
 
         def turn_x(i, tag, bufs):
-            x_ps[i] = psum.tile([P, GE, 2 * P], F32, name=tag, bufs=bufs)
+            x_ps[i] = psum.tile([P, 2 * GE, P], F32, name=tag, bufs=bufs)
             words = dv_sb[i][:].bitcast(F32)
             for g in range(GE):
                 for u in range(2):
-                    nc.tensor.transpose(x_ps[i][:, g, u:2 * P:2], words[:, 256 * g + u:256 * (g + 1):2], ident[:])
+                    nc.tensor.transpose(x_ps[i][:, 2 * g + u, :], words[:, 256 * g + u:256 * (g + 1):2], ident[:])
 
         def divide_x(i, dst):
             a = i // TILES
-            nc.vector.tensor_tensor(
-                out=dst[:, 0:E].rearrange("p (g r t) -> p g r t", r=P, t=4),
-                in0=x_ps[i][:].bitcast(BF16).rearrange("p g (r t) -> p g r t", t=4),
-                in1=recip[:, GE * a:GE * (a + 1), :].unsqueeze(2).to_broadcast([P, GE, P, 4]),
-                op=ALU.mult,
-            )
+            for g in range(GE):
+                nc.vector.tensor_tensor(
+                    out=dst[:, KP * g:KP * (g + 1)].rearrange("p (r u e) -> p r u e", u=2, e=2),
+                    in0=x_ps[i][:, 2 * g:2 * g + 2, :].bitcast(BF16).rearrange("p u (r e) -> p r u e", e=2),
+                    in1=recip[:, GE * a + g, :].rearrange("p (u e) -> p u e", e=2).unsqueeze(1).to_broadcast([P, P, 2, 2]),
+                    op=ALU.mult,
+                )
 
         def quantize(src, tag, lo, hi):
             width = src.shape[1] // 4
@@ -156,31 +159,33 @@ def tile_tactile_impedance_patches_k7_kernel(
         def saturate(i):
             th[i] = work.tile([P, PX], F32, name="th")
             for c in range(GP):
-                nc.scalar.activation(
-                    out=th[i][:, KP * c:KP * (c + 1)].rearrange("p (u m e) -> p u m e", u=2, e=2),
-                    in_=s_ps[i, c][:].rearrange("p (m u e) -> p u m e", u=2, e=2),
-                    func=ACT.Tanh,
-                )
+                nc.scalar.activation(out=group(th[i], c), in_=pick_words(s_ps[i, c][:]), func=ACT.Tanh)
 
-        def apply_gain(eng, i, lo, hi):
-            eng.tensor_tensor(
-                out=h_bf[i][:, lo:hi], in0=th[i][:, lo:hi], in1=gain32[i // TILES][:, lo:hi], op=ALU.mult
+        def gain_first_group(eng, i):
+            eng.tensor_tensor(out=h_bf[i][:, 0:KP], in0=th[i][:, 0:KP], in1=gain32[i // TILES][:], op=ALU.mult)
+
+        def gain_other_groups(i):
+            nc.vector.tensor_tensor(
+                out=by_words(h_bf[i][:, KP:PX]),
+                in0=by_words(th[i][:, KP:PX]),
+                in1=pick_words(gain_sb[i // TILES][:, KP:PX]),
+                op=ALU.mult,
             )
 
-        def apply_gain_by_group(i):
+        def gain_by_group(i):
             for c in range(GP):
-                cols = slice(KP * c, KP * (c + 1))
                 nc.vector.tensor_tensor(
-                    out=h_bf[i][:, cols].rearrange("p (u m e) -> p u m e", u=2, e=2),
-                    in0=th[i][:, cols].rearrange("p (u m e) -> p u m e", u=2, e=2),
-                    in1=gain_sb[i // TILES][:, cols].rearrange("p (m u e) -> p u m e", u=2, e=2),
+                    out=group(h_bf[i], c),
+                    in0=group(th[i], c),
+                    in1=pick_words(gain_sb[i // TILES][:, KP * c:KP * (c + 1)]),
                     op=ALU.mult,
                 )
 
         def turn_words(bank, slot, src, c):
-            words = src[:, KP * c:KP * (c + 1)].bitcast(F32)
+            words = src[:].bitcast(F32)
             for u in range(2):
-                nc.tensor.transpose(bank[:, 2 * slot + u, :], words[:, P * u:P * (u + 1)], ident[:])
+                first = P * u if c == 0 else 2 * P * (u + 1) + P * (c - 1)
+                nc.tensor.transpose(bank[:, 2 * slot + u, :], words[:, first:first + P], ident[:])
 
         def copy_words(dst, bank, lo, hi):
             nc.scalar.copy(
@@ -204,12 +209,12 @@ def tile_tactile_impedance_patches_k7_kernel(
 
         def add_rest(i):
             offs[i] = work.tile([P, N], F32, name="offs", bufs=4)
-            nc.vector.tensor_tensor(out=offs[i][:], in0=z_ps[i][:], in1=rest_sb[i // TILES][:], op=ALU.add)
+            nc.vector.tensor_tensor(out=offs[i][:], in0=z_ps[i][:], in1=rest_sb[i // TILES], op=ALU.add)
 
         def apply_stiff(i, eng, dst):
             a, j = divmod(i, TILES)
             y_sb[i] = dst
-            eng.tensor_tensor(out=dst, in0=offs[i][:], in1=stiff_sb[a][:], op=ALU.mult)
+            eng.tensor_tensor(out=dst, in0=offs[i][:], in1=stiff_sb[a], op=ALU.mult)
             nc.sync.dma_start(out=out_0[a, j * P:(j + 1) * P, :], in_=dst)
 
         def stiff_to_words(i):
@@ -217,7 +222,7 @@ def tile_tactile_impedance_patches_k7_kernel(
             nc.vector.tensor_tensor(
                 out=y_bf[i][:].rearrange("p (u m e) -> p u m e", u=2, e=2),
                 in0=offs[i][:].rearrange("p (m u e) -> p u m e", u=2, e=2),
-                in1=stiff_sb[i // TILES][:].rearrange("p (m u e) -> p u m e", u=2, e=2),
+                in1=stiff_sb[i // TILES].rearrange("p (m u e) -> p u m e", u=2, e=2),
                 op=ALU.mult,
             )
 
@@ -254,10 +259,13 @@ def tile_tactile_impedance_patches_k7_kernel(
         load_scales(r_planes[0], r_scales, slice(0, GE))
         for g in range(GE):
             load_r(0, g)
-        load_gain(0)
+        gain_sb = load_rows("gain_first", gain, 0, 1)
+        load_dv(AHEAD)
         vref_rest = load_vref(1, G)
         load_c(0)
-        load_rest(0)
+        load_dv(AHEAD + 1)
+        rest_sb = load_rows("rest", rest, 0, G)
+        stiff_sb = load_rows("stiff", stiff, 0, G)
         nc.vector.reciprocal(out=recip[:, 0:GE, :], in_=vref0[:, :, 0:4])
 
         bank_a, bank_b, mix, third, y_in = {}, {}, {}, {}, {}
@@ -317,19 +325,17 @@ def tile_tactile_impedance_patches_k7_kernel(
             if i > 0:
                 quantize_mix(i - 2, i - 1, -1)
         for s in range(0, last):
-            if live(s + 4):
-                load_dv(s + 4)
+            if s == 2:
+                gain_sb = {**gain_sb, **load_rows("gain_others", gain, 1, G)}
+            if s > 0 and live(s + 5):
+                load_dv(s + 5)
             nxt = s // TILES + 1
             if nxt < G and s % TILES == 1:
                 load_scales(r_planes[nxt % 2], r_scales, slice(GE * nxt, GE * (nxt + 1)))
                 for g in range(GE):
                     load_r(nxt, g)
-            if nxt < G and s % TILES == 0:
-                load_gain(nxt)
             if nxt < G and s % TILES == 3:
                 load_c(nxt)
-            if s > 0 and s % TILES == 0:
-                load_rest(s // TILES)
             if s == 2:
                 nc.vector.reciprocal(out=recip[:, GE:, :], in_=vref_rest[:, :, 0:4])
 
@@ -344,7 +350,7 @@ def tile_tactile_impedance_patches_k7_kernel(
             if live(ig):
                 h_bf[ig] = third[s - 1] if shared else new_third()
             if shared:
-                apply_gain(nc.gpsimd, ig, 0, SHARE)
+                gain_first_group(nc.gpsimd, ig)
             if ix >= AHEAD:
                 new_mix(s)
                 divide_x(ix, mix[s])
@@ -352,13 +358,15 @@ def tile_tactile_impedance_patches_k7_kernel(
                 add_rest(iz)
             if live(ih):
                 copy_hy(s, ih, iy)
+            if s % TILES == 0 and s > 0:
+                sort_gain(s // TILES, nc.scalar.copy)
             stage1(s)
             if shared:
-                apply_gain(nc.vector, ig, SHARE, PX)
+                gain_other_groups(ig)
             elif live(ig):
-                apply_gain_by_group(ig)
+                gain_by_group(ig)
             if s == 2:
-                sort_gain(0, 0, GP, nc.vector.tensor_copy)
+                sort_gain(0, nc.vector.tensor_copy)
             if live(iz):
                 stiff_on_vector(iz)
             if live(ih):
@@ -372,13 +380,12 @@ def tile_tactile_impedance_patches_k7_kernel(
                 saturate(s)
             if live(iz):
                 round_y(iz)
-            if s % TILES > 0 and nxt < G and s > 1:
-                sort_gain(nxt, 0 if s == 2 else s % TILES - 1, s % TILES, nc.scalar.copy)
 
         turn_hy(15, 13, 11, "bank_a", "bank_b", 1)
         stage1(15)
         h_bf[14] = new_third()
-        apply_gain(nc.vector, 14, 0, PX)
+        gain_first_group(nc.vector, 14)
+        gain_other_groups(14)
         new_mix(15)
         copy_hy(15, 13, 11)
         add_rest(12)
@@ -392,7 +399,7 @@ def tile_tactile_impedance_patches_k7_kernel(
         new_mix(16)
         copy_hy(16, 14, -1)
         h_bf[15] = new_third()
-        apply_gain_by_group(15)
+        gain_by_group(15)
         round_y(12)
         add_rest(13)
         quantize_mix(16, -1, 14)

@@ -23,6 +23,25 @@ GP = PX // KP
 TILES = T // P
 UNITS = G * TILES
 AHEAD = 4
+NO_TILE = -1
+
+
+def in_pair_order(ap):
+    return ap.rearrange("p (u m e) -> p u m e", u=2, e=2)
+
+
+def to_pair_order(ap):
+    return ap.rearrange("p (m u e) -> p u m e", u=2, e=2)
+
+
+def pixel_group(ap, c):
+    if c == 0:
+        return in_pair_order(ap[:, 0:KP])
+    return in_pair_order(ap[:, KP:PX])[:, :, P * (c - 1):P * c, :]
+
+
+def live(i):
+    return 0 <= i < UNITS
 
 
 def tile_tactile_impedance_patches_k7_kernel(
@@ -37,30 +56,20 @@ def tile_tactile_impedance_patches_k7_kernel(
 
         ident = keep.tile([P, P], F32, name="ident")
         make_identity(nc, ident[:])
-        warm = keep.tile([P, 8], F32, name="warm")
-        nc.vector.memset(warm[:, 0:1], 0.0)
-        nc.scalar.activation(out=warm[:, 4:5], in_=warm[:, 0:1], func=ACT.Tanh)
-
         r_planes, c_planes = [], []
-        for a in range(2):
-            r_planes.append(keep.tile([P, GE, PX], U8, name="r_plane%d" % a, align_bytes=64))
-            c_planes.append(keep.tile([P, GP, N], U8, name="c_plane%d" % a, align_bytes=64))
-        for a in range(2):
-            nc.vector.memset(r_planes[a][:].rearrange("p g n -> p (g n)").bitcast(I32), 0)
-            nc.vector.memset(c_planes[a][:].rearrange("p g n -> p (g n)").bitcast(I32), 0)
+        for k in range(2):
+            r_planes.append(keep.tile([P, GE, PX], U8, name="r_plane%d" % k, align_bytes=64))
+            c_planes.append(keep.tile([P, GP, N], U8, name="c_plane%d" % k, align_bytes=64))
+        for k in range(2):
+            nc.vector.memset(r_planes[k][:].rearrange("p g n -> p (g n)").bitcast(I32), 0)
+            nc.vector.memset(c_planes[k][:].rearrange("p g n -> p (g n)").bitcast(I32), 0)
 
-        def by_words(ap):
-            return ap.rearrange("p (u m e) -> p u m e", u=2, e=2)
+        recip = keep.tile([P, G * GE, 4], F32, name="recip")
 
-        def pick_words(ap):
-            return ap.rearrange("p (m u e) -> p u m e", u=2, e=2)
+        r_sb, c_sb, gain_sb, gain_sorted, rest_sb, stiff_sb, y_scales = {}, {}, {}, {}, {}, {}, {}
+        dv_sb, x_ps, x_ops, s_ps, th, h_bf, h_ops, z_ps, offs, y_sb, y_bf = {}, {}, {}, {}, {}, {}, {}, {}, {}, {}, {}
+        bank_a, bank_b, mix, third, y_in = {}, {}, {}, {}, {}
 
-        def group(ap, c):
-            if c == 0:
-                return by_words(ap[:, 0:KP])
-            return by_words(ap[:, KP:PX])[:, :, P * (c - 1):P * c, :]
-
-        dv_sb, r_sb, c_sb = {}, {}, {}
 
         def load_dv(i):
             a, j = divmod(i, TILES)
@@ -73,8 +82,6 @@ def tile_tactile_impedance_patches_k7_kernel(
                 nc.sync.dma_start(out=rows[:, :, 0:4], in_=vref[lo:hi].rearrange("a (g p t) -> p (a g) t", g=GE, t=4))
             return rows
 
-        recip = keep.tile([P, G * GE, 4], F32, name="recip")
-
         def load_scales(plane, scales, groups):
             for q in range(4):
                 nc.sync.dma_start(
@@ -82,47 +89,45 @@ def tile_tactile_impedance_patches_k7_kernel(
                     in_=scales[groups, 4 * q:4 * q + 4, :].rearrange("g r n -> r g n").bitcast(I32),
                 )
 
-        def load_r(a, g):
-            r_sb[a, g] = work.tile([P, 2 * PX], U8, name="r_words%d" % g, align_bytes=64)
-            nc.sync.dma_start(out=r_sb[a, g][:].bitcast(I32), in_=r_words[GE * a + g].bitcast(I32))
-
-        def load_rows(name, vector, lo, hi):
-            width = vector.shape[1]
-            rows = keep.tile([P, (hi - lo) * width], BF16, name=name)
-            nc.sync.dma_start(out=rows[:], in_=vector[lo:hi].rearrange("a n -> (a n)").partition_broadcast(P))
-            return {a: rows[:, width * (a - lo):width * (a - lo + 1)] for a in range(lo, hi)}
-
-        def sort_gain(a, copy):
-            gain32[a] = work.tile([P, KP], F32, name="gain32")
-            copy(out=by_words(gain32[a][:]), in_=pick_words(gain_sb[a][:, 0:KP]))
+        def load_r(a):
+            load_scales(r_planes[a % 2], r_scales, slice(GE * a, GE * (a + 1)))
+            for g in range(GE):
+                r_sb[a, g] = work.tile([P, 2 * PX], U8, name="r_words%d" % g, align_bytes=64)
+                nc.sync.dma_start(out=r_sb[a, g][:].bitcast(I32), in_=r_words[GE * a + g].bitcast(I32))
 
         def load_c(a):
             load_scales(c_planes[a % 2], c_scales, slice(GP * a, GP * (a + 1)))
-            c_sb[a] = keep.tile([P, GP, 2 * N], U8, name="c%d" % a, align_bytes=64)
+            c_sb[a] = work.tile([P, GP, 2 * N], U8, name="c_words", align_bytes=64)
             nc.sync.dma_start(
                 out=c_sb[a][:].bitcast(I32),
                 in_=c_words[GP * a:GP * (a + 1)].rearrange("g p n -> p g n").bitcast(I32),
             )
 
-        x_ps, x_bf, x_q, x_s, s_ps, th, h_bf = {}, {}, {}, {}, {}, {}, {}
-        h_qa, h_sa, h_qb, h_sb, z_ps, y_sb, y_bf, y_s = {}, {}, {}, {}, {}, {}, {}, {}
-        offs, h_q, gain32 = {}, {}, {}
+        def load_row(name, row):
+            spread = work.tile([P, row.shape[0]], BF16, name=name)
+            nc.sync.dma_start(out=spread[:], in_=row.partition_broadcast(P))
+            return spread
 
-        def live(i):
-            return 0 <= i < UNITS
+        def load_offsets(a):
+            rest_sb[a] = load_row("rest_row", rest[a])
+            stiff_sb[a] = load_row("stiff_row", stiff[a])
+
 
         def turn_x(i, tag, bufs):
             x_ps[i] = psum.tile([P, 2 * GE, P], F32, name=tag, bufs=bufs)
-            words = dv_sb[i][:].bitcast(F32)
+            pairs = dv_sb[i][:].bitcast(F32)
             for g in range(GE):
                 for u in range(2):
-                    nc.tensor.transpose(x_ps[i][:, 2 * g + u, :], words[:, 256 * g + u:256 * (g + 1):2], ident[:])
+                    nc.tensor.transpose(x_ps[i][:, 2 * g + u, :], pairs[:, 256 * g + u:256 * (g + 1):2], ident[:])
 
-        def divide_x(i, dst):
+        def new_mix(s):
+            mix[s] = work.tile([P, 4 * KP], BF16, name="mix", align_bytes=64, bufs=4)
+
+        def divide_x(i, s):
             a = i // TILES
             for g in range(GE):
                 nc.vector.tensor_tensor(
-                    out=dst[:, KP * g:KP * (g + 1)].rearrange("p (r u e) -> p r u e", u=2, e=2),
+                    out=mix[s][:, KP * g:KP * (g + 1)].rearrange("p (r u e) -> p r u e", u=2, e=2),
                     in0=x_ps[i][:, 2 * g:2 * g + 2, :].bitcast(BF16).rearrange("p u (r e) -> p r u e", e=2),
                     in1=recip[:, GE * a + g, :].rearrange("p (u e) -> p u e", e=2).unsqueeze(1).to_broadcast([P, P, 2, 2]),
                     op=ALU.mult,
@@ -130,68 +135,93 @@ def tile_tactile_impedance_patches_k7_kernel(
 
         def quantize(src, tag, lo, hi):
             width = src.shape[1] // 4
-            codes = work.tile([P, width], U32, name=tag + "_q", align_bytes=64, bufs=4)
-            scales = work.tile([P, width], U8, name=tag + "_s", align_bytes=64, bufs=4)
+            codes = work.tile([P, width], U32, name=tag + "_codes", align_bytes=64, bufs=4)
+            scales = work.tile([P, width], U8, name=tag + "_scales", align_bytes=64, bufs=4)
             nc.vector.quantize_mx(
                 out=codes[:, P * lo:P * hi].bitcast(FP8X4), scales=scales[:, P * lo:P * hi], in_=src[:, KP * lo:KP * hi]
             )
             return [(codes[:, P * k:P * (k + 1)].bitcast(FP8X4), scales[:, P * k:P * (k + 1)]) for k in range(width // P)]
 
-        def stage1_pass(i, c, g):
-            a = i // TILES
-            if g == 0:
-                s_ps[i, c] = psum.tile([P, KP], F32, name="s_ps%d" % c)
-            nc.tensor.matmul_mx(
-                out=s_ps[i, c][:],
-                lhsT=x_q[i][g][0],
-                lhsT_scale=x_q[i][g][1],
-                rhs=r_sb[a, g][:, 2 * KP * c:2 * KP * (c + 1)].bitcast(FP4X4),
-                rhs_scale=r_planes[a % 2][:, g, KP * c:KP * (c + 1)],
-                start=(g == 0),
-                stop=(g == GE - 1),
-            )
+        def quantize_mix(s, ix, ih):
+            ops = quantize(mix[s], "mix", 0 if live(ix) else 2, 4 if live(ih) else 2)
+            x_ops[ix], h_ops[ih] = ops[0:2], ops[2:4]
+
 
         def stage1(i):
+            a = i // TILES
             for c in range(GP):
+                s_ps[i, c] = psum.tile([P, KP], F32, name="s_ps%d" % c)
                 for g in range(GE):
-                    stage1_pass(i, c, g)
+                    nc.tensor.matmul_mx(
+                        out=s_ps[i, c][:],
+                        lhsT=x_ops[i][g][0],
+                        lhsT_scale=x_ops[i][g][1],
+                        rhs=r_sb[a, g][:, 2 * KP * c:2 * KP * (c + 1)].bitcast(FP4X4),
+                        rhs_scale=r_planes[a % 2][:, g, KP * c:KP * (c + 1)],
+                        start=(g == 0),
+                        stop=(g == GE - 1),
+                    )
 
         def saturate(i):
             th[i] = work.tile([P, PX], F32, name="th")
             for c in range(GP):
-                nc.scalar.activation(out=group(th[i], c), in_=pick_words(s_ps[i, c][:]), func=ACT.Tanh)
+                nc.scalar.activation(out=pixel_group(th[i], c), in_=to_pair_order(s_ps[i, c][:]), func=ACT.Tanh)
+
+        def sort_gain(a, copy):
+            gain_sorted[a] = work.tile([P, KP], F32, name="gain_sorted")
+            copy(out=in_pair_order(gain_sorted[a][:]), in_=to_pair_order(gain_sb[a][:, 0:KP]))
+
+        def new_third():
+            fresh = work.tile([P, PX], BF16, name="third", align_bytes=64, bufs=4)
+            return fresh
 
         def gain_first_group(eng, i):
-            eng.tensor_tensor(out=h_bf[i][:, 0:KP], in0=th[i][:, 0:KP], in1=gain32[i // TILES][:], op=ALU.mult)
+            eng.tensor_tensor(out=h_bf[i][:, 0:KP], in0=th[i][:, 0:KP], in1=gain_sorted[i // TILES][:], op=ALU.mult)
 
         def gain_other_groups(i):
             nc.vector.tensor_tensor(
-                out=by_words(h_bf[i][:, KP:PX]),
-                in0=by_words(th[i][:, KP:PX]),
-                in1=pick_words(gain_sb[i // TILES][:, KP:PX]),
+                out=in_pair_order(h_bf[i][:, KP:PX]),
+                in0=in_pair_order(th[i][:, KP:PX]),
+                in1=to_pair_order(gain_sb[i // TILES][:, KP:PX]),
                 op=ALU.mult,
             )
 
         def gain_by_group(i):
             for c in range(GP):
                 nc.vector.tensor_tensor(
-                    out=group(h_bf[i], c),
-                    in0=group(th[i], c),
-                    in1=pick_words(gain_sb[i // TILES][:, KP * c:KP * (c + 1)]),
+                    out=pixel_group(h_bf[i], c),
+                    in0=pixel_group(th[i], c),
+                    in1=to_pair_order(gain_sb[i // TILES][:, KP * c:KP * (c + 1)]),
                     op=ALU.mult,
                 )
 
-        def turn_words(bank, slot, src, c):
-            words = src[:].bitcast(F32)
+        def turn_pairs(bank, slot, src, c):
+            pairs = src[:].bitcast(F32)
             for u in range(2):
                 first = P * u if c == 0 else 2 * P * (u + 1) + P * (c - 1)
-                nc.tensor.transpose(bank[:, 2 * slot + u, :], words[:, first:first + P], ident[:])
+                nc.tensor.transpose(bank[:, 2 * slot + u, :], pairs[:, first:first + P], ident[:])
 
-        def copy_words(dst, bank, lo, hi):
+        def copy_pairs(dst, bank, lo, hi):
             nc.scalar.copy(
                 out=dst.bitcast(F32).rearrange("p (g r u) -> p g r u", r=P, u=2),
                 in_=bank[:, 2 * lo:2 * hi, :].rearrange("p (g u) r -> p g r u", u=2),
             )
+
+        def turn_h(s, i, tag_a, tag_b, bufs):
+            bank_a[s] = psum.tile([P, 4, P], F32, name=tag_a, bufs=bufs)
+            turn_pairs(bank_a[s], 0, h_bf[i], 0)
+            turn_pairs(bank_a[s], 1, h_bf[i], 1)
+            bank_b[s] = psum.tile([P, 4, P], F32, name=tag_b, bufs=bufs)
+            turn_pairs(bank_b[s], 0, h_bf[i], 2)
+
+        def copy_h(s):
+            copy_pairs(mix[s][:, 2 * KP:4 * KP], bank_a[s], 0, 2)
+            third[s] = new_third()
+            copy_pairs(third[s][:, 0:KP], bank_b[s], 0, 1)
+
+        def quantize_third(s, i):
+            h_ops[i] = h_ops[i] + quantize(third[s][:, 0:KP], "third", 0, 1)
+
 
         def stage2(i, tag):
             a = i // TILES
@@ -199,8 +229,8 @@ def tile_tactile_impedance_patches_k7_kernel(
             for g in range(GP):
                 nc.tensor.matmul_mx(
                     out=z_ps[i][:],
-                    lhsT=h_q[i][g][0],
-                    lhsT_scale=h_q[i][g][1],
+                    lhsT=h_ops[i][g][0],
+                    lhsT_scale=h_ops[i][g][1],
                     rhs=c_sb[a][:, g, :].bitcast(FP4X4),
                     rhs_scale=c_planes[a % 2][:, g, :],
                     start=(g == 0),
@@ -208,218 +238,187 @@ def tile_tactile_impedance_patches_k7_kernel(
                 )
 
         def add_rest(i):
-            offs[i] = work.tile([P, N], F32, name="offs", bufs=4)
-            nc.vector.tensor_tensor(out=offs[i][:], in0=z_ps[i][:], in1=rest_sb[i // TILES], op=ALU.add)
+            offs[i] = work.tile([P, N], F32, name="offs")
+            nc.vector.tensor_tensor(out=offs[i][:], in0=z_ps[i][:], in1=rest_sb[i // TILES][:], op=ALU.add)
 
-        def apply_stiff(i, eng, dst):
+        def apply_stiff(i):
             a, j = divmod(i, TILES)
-            y_sb[i] = dst
-            eng.tensor_tensor(out=dst, in0=offs[i][:], in1=stiff_sb[a], op=ALU.mult)
-            nc.sync.dma_start(out=out_0[a, j * P:(j + 1) * P, :], in_=dst)
-
-        def stiff_to_words(i):
-            y_bf[i] = work.tile([P, N], BF16, name="y_bf", bufs=3)
-            nc.vector.tensor_tensor(
-                out=y_bf[i][:].rearrange("p (u m e) -> p u m e", u=2, e=2),
-                in0=offs[i][:].rearrange("p (m u e) -> p u m e", u=2, e=2),
-                in1=stiff_sb[i // TILES].rearrange("p (m u e) -> p u m e", u=2, e=2),
-                op=ALU.mult,
-            )
+            y_sb[i] = work.tile([P, N], F32, name="y_t", bufs=4)
+            nc.vector.tensor_tensor(out=y_sb[i][:], in0=offs[i][:], in1=stiff_sb[a][:], op=ALU.mult)
+            nc.sync.dma_start(out=out_0[a, j * P:(j + 1) * P, :], in_=y_sb[i][:])
 
         def round_y(i):
-            y_bf[i] = work.tile([P, N], BF16, name="y_bf", bufs=3)
-            nc.scalar.copy(
-                out=y_bf[i][:].rearrange("p (u m e) -> p u m e", u=2, e=2),
-                in_=y_sb[i].rearrange("p (m u e) -> p u m e", u=2, e=2),
+            y_bf[i] = work.tile([P, N], BF16, name="y_bf")
+            nc.scalar.copy(out=in_pair_order(y_bf[i][:]), in_=to_pair_order(y_sb[i][:]))
+
+        def apply_stiff_rounded(i):
+            y_bf[i] = work.tile([P, N], BF16, name="y_bf")
+            nc.vector.tensor_tensor(
+                out=in_pair_order(y_bf[i][:]),
+                in0=to_pair_order(offs[i][:]),
+                in1=to_pair_order(stiff_sb[i // TILES][:]),
+                op=ALU.mult,
             )
-
-        def quantize_y(i, src):
-            a, j = divmod(i, TILES)
-            width = src.shape[1] // 4
-            if j == 0:
-                y_s[a] = work.tile([P, T], U8, name="y_s", align_bytes=64)
-            y_q = work.tile([P, width], U32, name="y_q", align_bytes=64, bufs=4)
-            nc.vector.quantize_mx(out=y_q[:].bitcast(FP8X4), scales=y_s[a][:, P * j:P * j + width], in_=src)
-            nc.sync.dma_start(
-                out=out_1[0, :, P * i:P * i + width, :].rearrange("p m t -> p (m t)").bitcast(I32),
-                in_=y_q[:].bitcast(I32),
-            )
-            if P * j + width == T:
-                for q in range(4):
-                    queue = nc.scalar if a == G - 1 and q % 2 == 1 else nc.sync
-                    queue.dma_start(
-                        out=out_2[0, 4 * q:4 * q + 4, T * a:T * (a + 1)].bitcast(I32),
-                        in_=y_s[a][32 * q:32 * q + 4, :].bitcast(I32),
-                    )
-
-        load_dv(0)
-        vref0 = load_vref(0, 1)
-        for i in range(1, AHEAD):
-            load_dv(i)
-        load_scales(r_planes[0], r_scales, slice(0, GE))
-        for g in range(GE):
-            load_r(0, g)
-        gain_sb = load_rows("gain_first", gain, 0, 1)
-        load_dv(AHEAD)
-        vref_rest = load_vref(1, G)
-        load_c(0)
-        load_dv(AHEAD + 1)
-        rest_sb = load_rows("rest", rest, 0, G)
-        stiff_sb = load_rows("stiff", stiff, 0, G)
-        nc.vector.reciprocal(out=recip[:, 0:GE, :], in_=vref0[:, :, 0:4])
-
-        bank_a, bank_b, mix, third, y_in = {}, {}, {}, {}, {}
-
-        def turn_hy(key, ih, iy, tag_a, tag_b, bufs):
-            if live(ih):
-                bank_a[key] = psum.tile([P, 4, P], F32, name=tag_a, bufs=bufs)
-                turn_words(bank_a[key], 0, h_bf[ih], 0)
-                turn_words(bank_a[key], 1, h_bf[ih], 1)
-            bank_b[key] = psum.tile([P, 4, P], F32, name=tag_b, bufs=bufs)
-            if live(ih):
-                turn_words(bank_b[key], 0, h_bf[ih], 2)
-            if live(iy):
-                turn_words(bank_b[key], 1, y_bf[iy], 0)
-
-        def new_mix(key):
-            mix[key] = work.tile([P, 4 * KP], BF16, name="mix", align_bytes=64, bufs=4)
-
-        def new_third():
-            fresh = work.tile([P, PX], BF16, name="third", align_bytes=64, bufs=4)
-            return fresh
 
         def copy_y(i, bank, lo, hi):
             if i % 2 == 0:
                 y_in[i // 2] = work.tile([P, 2 * KP], BF16, name="y_in", align_bytes=64)
-            copy_words(y_in[i // 2][:, KP * (i % 2):KP * (i % 2 + hi - lo)], bank, lo, hi)
+            copy_pairs(y_in[i // 2][:, KP * (i % 2):KP * (i % 2 + hi - lo)], bank, lo, hi)
 
-        def copy_hy(key, ih, iy):
-            copy_words(mix[key][:, 2 * KP:4 * KP], bank_a[key], 0, 2)
-            third[key] = new_third()
-            copy_words(third[key][:, 0:KP], bank_b[key], 0, 1)
-            if live(iy):
-                copy_y(iy, bank_b[key], 1, 2)
-
-        def quantize_mix(key, ix, ih):
-            ops = quantize(mix[key], "a", 0 if live(ix) else 2, 4 if live(ih) else 2)
-            x_q[ix], h_q[ih] = ops[0:2], ops[2:4]
-
-        def quantize_third(key, ih):
-            h_q[ih] = h_q[ih] + quantize(third[key][:, 0:KP], "b", 0, 1)
-
-        def turn_y_pair(i, tag):
+        def turn_and_copy_two_y(i, tag):
             bank = psum.tile([P, 4, P], F32, name=tag)
-            turn_words(bank, 0, y_bf[i], 0)
-            turn_words(bank, 1, y_bf[i + 1], 0)
+            turn_pairs(bank, 0, y_bf[i], 0)
+            turn_pairs(bank, 1, y_bf[i + 1], 0)
             copy_y(i, bank, 0, 2)
 
-        def stiff_on_vector(i):
-            y_own = work.tile([P, N], F32, name="y_own", bufs=4)
-            apply_stiff(i, nc.vector, y_own[:])
+        def quantize_y(i):
+            a, j = divmod(i, TILES)
+            if j == 0:
+                y_scales[a] = work.tile([P, T], U8, name="y_scales", align_bytes=64)
+            y_codes = work.tile([P, 2 * P], U32, name="y_codes", align_bytes=64)
+            nc.vector.quantize_mx(
+                out=y_codes[:].bitcast(FP8X4), scales=y_scales[a][:, P * j:P * (j + 2)], in_=y_in[i // 2][:]
+            )
+            nc.sync.dma_start(
+                out=out_1[0, :, P * i:P * (i + 2), :].rearrange("p m t -> p (m t)").bitcast(I32),
+                in_=y_codes[:].bitcast(I32),
+            )
+            if j + 2 == TILES:
+                for q in range(4):
+                    queue = nc.scalar if a == G - 1 and q % 2 == 1 else nc.sync
+                    queue.dma_start(
+                        out=out_2[0, 4 * q:4 * q + 4, T * a:T * (a + 1)].bitcast(I32),
+                        in_=y_scales[a][32 * q:32 * q + 4, :].bitcast(I32),
+                    )
+
+
+        load_dv(0)
+        vref_first = load_vref(0, 1)
+        for i in range(1, AHEAD):
+            load_dv(i)
+        load_r(0)
+        gain_sb[0] = load_row("gain_row", gain[0])
+        load_dv(AHEAD)
+        vref_others = load_vref(1, G)
+        load_c(0)
+        load_dv(AHEAD + 1)
+        load_offsets(0)
+        nc.vector.reciprocal(out=recip[:, 0:GE, :], in_=vref_first[:, :, 0:4])
+
+        for i, (tag, bufs) in enumerate([("x_ps", 2), ("x_ps", 2), ("bank_a", 1), ("bank_b", 1)]):
+            turn_x(i, tag, bufs)
+            new_mix(i - 1)
+            divide_x(i, i - 1)
+            if i > 0:
+                quantize_mix(i - 2, i - 1, NO_TILE)
 
         last = UNITS - 1
-        for i in range(AHEAD):
-            turn_x(i, *[("x_ps", 2), ("x_ps", 2), ("bank_a", 1), ("bank_b", 1)][i])
-            new_mix(i - 1)
-            divide_x(i, mix[i - 1])
-            if i > 0:
-                quantize_mix(i - 2, i - 1, -1)
-        for s in range(0, last):
-            if s == 2:
-                gain_sb = {**gain_sb, **load_rows("gain_others", gain, 1, G)}
+        for s in range(last):
+            nxt, phase = s // TILES + 1, s % TILES
             if s > 0 and live(s + 5):
                 load_dv(s + 5)
-            nxt = s // TILES + 1
-            if nxt < G and s % TILES == 1:
-                load_scales(r_planes[nxt % 2], r_scales, slice(GE * nxt, GE * (nxt + 1)))
-                for g in range(GE):
-                    load_r(nxt, g)
-            if nxt < G and s % TILES == 3:
+            if nxt < G and phase == 1:
+                load_r(nxt)
+            if nxt < G and phase == 2:
+                gain_sb[nxt] = load_row("gain_row", gain[nxt])
+            if nxt < G and phase == 3:
                 load_c(nxt)
-            if s == 2:
-                nc.vector.reciprocal(out=recip[:, GE:, :], in_=vref_rest[:, :, 0:4])
+            if s > 0 and phase == 0:
+                load_offsets(s // TILES)
+            if s == AHEAD - 2:
+                nc.vector.reciprocal(out=recip[:, GE:, :], in_=vref_others[:, :, 0:4])
 
             ix, ig, ih, iz, iy = s + 1, s - 1, s - 2, s - 3, s - 4
             shared = s - 1 in third
             if live(ih):
-                turn_hy(s, ih, -1, "bank_a", "bank_b", 1)
+                turn_h(s, ih, "bank_a", "bank_b", 1)
             if AHEAD <= s + 2 < UNITS:
                 turn_x(s + 2, "x_ps", 2)
             if live(iy):
-                turn_words(bank_b[s], 1, y_bf[iy], 0)
+                turn_pairs(bank_b[s], 1, y_bf[iy], 0)
             if live(ig):
                 h_bf[ig] = third[s - 1] if shared else new_third()
             if shared:
                 gain_first_group(nc.gpsimd, ig)
             if ix >= AHEAD:
                 new_mix(s)
-                divide_x(ix, mix[s])
+                divide_x(ix, s)
             if live(iz):
                 add_rest(iz)
             if live(ih):
-                copy_hy(s, ih, iy)
-            if s % TILES == 0 and s > 0:
+                copy_h(s)
+            if live(iy):
+                copy_y(iy, bank_b[s], 1, 2)
+            if s > 0 and phase == 0:
                 sort_gain(s // TILES, nc.scalar.copy)
             stage1(s)
             if shared:
                 gain_other_groups(ig)
             elif live(ig):
                 gain_by_group(ig)
-            if s == 2:
+            if ih == 0:
                 sort_gain(0, nc.vector.tensor_copy)
             if live(iz):
-                stiff_on_vector(iz)
+                apply_stiff(iz)
             if live(ih):
                 quantize_mix(s, ix, ih)
             if live(iy) and iy % 2 == 1:
-                quantize_y(iy - 1, y_in[iy // 2][:])
+                quantize_y(iy - 1)
             if live(ih):
                 quantize_third(s, ih)
                 stage2(ih, "z_ps")
-            if live(s):
-                saturate(s)
+            saturate(s)
             if live(iz):
                 round_y(iz)
 
-        turn_hy(15, 13, 11, "bank_a", "bank_b", 1)
-        stage1(15)
-        h_bf[14] = new_third()
-        gain_first_group(nc.vector, 14)
-        gain_other_groups(14)
-        new_mix(15)
-        copy_hy(15, 13, 11)
-        add_rest(12)
-        quantize_mix(15, -1, 13)
-        quantize_third(15, 13)
-        saturate(15)
-        turn_hy(16, 14, -1, "x_ps", "x_ps", 2)
-        stage2(13, "z_ps")
-        stiff_on_vector(12)
-        quantize_y(10, y_in[5][:])
-        new_mix(16)
-        copy_hy(16, 14, -1)
-        h_bf[15] = new_third()
-        gain_by_group(15)
-        round_y(12)
-        add_rest(13)
-        quantize_mix(16, -1, 14)
-        quantize_third(16, 14)
-        turn_hy(17, 15, -1, "bank_a", "bank_b", 1)
-        stage2(14, "s_ps0")
-        new_mix(17)
-        copy_hy(17, 15, -1)
-        stiff_on_vector(13)
-        round_y(13)
-        quantize_mix(17, -1, 15)
-        quantize_third(17, 15)
-        stage2(15, "s_ps1")
-        turn_y_pair(12, "bank_a")
-        add_rest(14)
-        add_rest(15)
-        stiff_on_vector(14)
-        round_y(14)
-        stiff_to_words(15)
-        quantize_y(12, y_in[6][:])
-        turn_y_pair(14, "bank_b")
-        stiff_on_vector(15)
-        quantize_y(14, y_in[7][:])
+        a_tile, b_tile, c_tile = last - 2, last - 1, last
+        s = last
+        turn_h(s, a_tile, "bank_a", "bank_b", 1)
+        turn_pairs(bank_b[s], 1, y_bf[last - 4], 0)
+        stage1(c_tile)
+        h_bf[b_tile] = new_third()
+        gain_first_group(nc.vector, b_tile)
+        gain_other_groups(b_tile)
+        new_mix(s)
+        copy_h(s)
+        copy_y(last - 4, bank_b[s], 1, 2)
+        add_rest(last - 3)
+        quantize_mix(s, NO_TILE, a_tile)
+        quantize_third(s, a_tile)
+        saturate(c_tile)
+
+        s = last + 1
+        turn_h(s, b_tile, "x_ps", "x_ps", 2)
+        stage2(a_tile, "z_ps")
+        apply_stiff(last - 3)
+        quantize_y(last - 5)
+        new_mix(s)
+        copy_h(s)
+        h_bf[c_tile] = new_third()
+        gain_by_group(c_tile)
+        round_y(last - 3)
+        quantize_mix(s, NO_TILE, b_tile)
+        quantize_third(s, b_tile)
+        add_rest(a_tile)
+
+        s = last + 2
+        turn_h(s, c_tile, "bank_a", "bank_b", 1)
+        stage2(b_tile, "s_ps0")
+        new_mix(s)
+        copy_h(s)
+        quantize_mix(s, NO_TILE, c_tile)
+        apply_stiff(a_tile)
+        round_y(a_tile)
+        quantize_third(s, c_tile)
+        stage2(c_tile, "s_ps1")
+
+        turn_and_copy_two_y(last - 3, "bank_a")
+        add_rest(b_tile)
+        add_rest(c_tile)
+        apply_stiff(b_tile)
+        round_y(b_tile)
+        apply_stiff_rounded(c_tile)
+        quantize_y(last - 3)
+        turn_and_copy_two_y(b_tile, "bank_b")
+        apply_stiff(c_tile)
+        quantize_y(b_tile)

from contextlib import ExitStack

import concourse.mybir as mybir
from concourse.masks import make_identity

G, T, E, PX, N = 4, 512, 1024, 1536, 512
FLOPS = 2 * G * T * (E * PX + PX * N)

F32 = mybir.dt.float32
BF16 = mybir.dt.bfloat16
I32 = mybir.dt.int32
U32 = mybir.dt.uint32
U8 = mybir.dt.uint8
FP8X4 = mybir.dt.float8_e4m3fn_x4
FP4X4 = mybir.dt.float4_e2m1fn_x4
ALU = mybir.AluOpType
ACT = mybir.ActivationFunctionType

P = 128
KP = 512
GE = E // KP
GP = PX // KP
TILES = T // P
UNITS = G * TILES
AHEAD = 4
NO_TILE = -1


def in_pair_order(ap):
    return ap.rearrange("p (u m e) -> p u m e", u=2, e=2)


def to_pair_order(ap):
    return ap.rearrange("p (m u e) -> p u m e", u=2, e=2)


def pixel_group(ap, c):
    if c == 0:
        return in_pair_order(ap[:, 0:KP])
    return in_pair_order(ap[:, KP:PX])[:, :, P * (c - 1):P * c, :]


def live(i):
    return 0 <= i < UNITS


def tile_tactile_impedance_patches_k7_kernel(
    tc, dv, vref, r_words, r_scales, gain, c_words, c_scales, rest, stiff, out_0, out_1, out_2
):
    nc = tc.nc
    with ExitStack() as ctx:
        keep = ctx.enter_context(tc.tile_pool(name="keep", bufs=1))
        work = ctx.enter_context(tc.tile_pool(name="work", bufs=2))
        psum = ctx.enter_context(tc.psum_pool(name="psum", bufs=1))
        ctx.enter_context(tc.manual_schedule())

        ident = keep.tile([P, P], F32, name="ident")
        make_identity(nc, ident[:])
        r_planes, c_planes = [], []
        for k in range(2):
            r_planes.append(keep.tile([P, GE, PX], U8, name="r_plane%d" % k, align_bytes=64))
            c_planes.append(keep.tile([P, GP, N], U8, name="c_plane%d" % k, align_bytes=64))
        for k in range(2):
            nc.vector.memset(r_planes[k][:].rearrange("p g n -> p (g n)").bitcast(I32), 0)
            nc.vector.memset(c_planes[k][:].rearrange("p g n -> p (g n)").bitcast(I32), 0)

        recip = keep.tile([P, G * GE, 4], F32, name="recip")

        r_sb, c_sb, gain_sb, gain_sorted, rest_sb, stiff_sb, y_scales = {}, {}, {}, {}, {}, {}, {}
        dv_sb, x_ps, x_ops, s_ps, th, h_bf, h_ops, z_ps, offs, y_sb, y_bf = {}, {}, {}, {}, {}, {}, {}, {}, {}, {}, {}
        bank_a, bank_b, mix, third, y_in = {}, {}, {}, {}, {}


        def load_dv(i):
            a, j = divmod(i, TILES)
            dv_sb[i] = work.tile([P, E], BF16, name="dv_t", bufs=6)
            nc.sync.dma_start(out=dv_sb[i][:], in_=dv[a, j * P:(j + 1) * P, :])

        def load_vref(lo, hi):
            rows = keep.tile([P, GE * (hi - lo), 16], BF16, name="vref%d" % lo)
            with nc.allow_non_contiguous_dma("four values a partition and group"):
                nc.sync.dma_start(out=rows[:, :, 0:4], in_=vref[lo:hi].rearrange("a (g p t) -> p (a g) t", g=GE, t=4))
            return rows

        def load_scales(plane, scales, groups):
            for q in range(4):
                nc.sync.dma_start(
                    out=plane[32 * q:32 * q + 4, :, :].bitcast(I32),
                    in_=scales[groups, 4 * q:4 * q + 4, :].rearrange("g r n -> r g n").bitcast(I32),
                )

        def load_r(a):
            load_scales(r_planes[a % 2], r_scales, slice(GE * a, GE * (a + 1)))
            for g in range(GE):
                r_sb[a, g] = work.tile([P, 2 * PX], U8, name="r_words%d" % g, align_bytes=64)
                nc.sync.dma_start(out=r_sb[a, g][:].bitcast(I32), in_=r_words[GE * a + g].bitcast(I32))

        def load_c(a):
            load_scales(c_planes[a % 2], c_scales, slice(GP * a, GP * (a + 1)))
            c_sb[a] = work.tile([P, GP, 2 * N], U8, name="c_words", align_bytes=64)
            nc.sync.dma_start(
                out=c_sb[a][:].bitcast(I32),
                in_=c_words[GP * a:GP * (a + 1)].rearrange("g p n -> p g n").bitcast(I32),
            )

        def load_row(name, row):
            spread = work.tile([P, row.shape[0]], BF16, name=name)
            nc.sync.dma_start(out=spread[:], in_=row.partition_broadcast(P))
            return spread

        def load_offsets(a):
            rest_sb[a] = load_row("rest_row", rest[a])
            stiff_sb[a] = load_row("stiff_row", stiff[a])


        def turn_x(i, tag, bufs):
            x_ps[i] = psum.tile([P, 2 * GE, P], F32, name=tag, bufs=bufs)
            pairs = dv_sb[i][:].bitcast(F32)
            for g in range(GE):
                for u in range(2):
                    nc.tensor.transpose(x_ps[i][:, 2 * g + u, :], pairs[:, 256 * g + u:256 * (g + 1):2], ident[:])

        def new_mix(s):
            mix[s] = work.tile([P, 4 * KP], BF16, name="mix", align_bytes=64, bufs=4)

        def divide_x(i, s):
            a = i // TILES
            for g in range(GE):
                nc.vector.tensor_tensor(
                    out=mix[s][:, KP * g:KP * (g + 1)].rearrange("p (r u e) -> p r u e", u=2, e=2),
                    in0=x_ps[i][:, 2 * g:2 * g + 2, :].bitcast(BF16).rearrange("p u (r e) -> p r u e", e=2),
                    in1=recip[:, GE * a + g, :].rearrange("p (u e) -> p u e", e=2).unsqueeze(1).to_broadcast([P, P, 2, 2]),
                    op=ALU.mult,
                )

        def quantize(src, tag, lo, hi):
            width = src.shape[1] // 4
            codes = work.tile([P, width], U32, name=tag + "_codes", align_bytes=64, bufs=4)
            scales = work.tile([P, width], U8, name=tag + "_scales", align_bytes=64, bufs=4)
            nc.vector.quantize_mx(
                out=codes[:, P * lo:P * hi].bitcast(FP8X4), scales=scales[:, P * lo:P * hi], in_=src[:, KP * lo:KP * hi]
            )
            return [(codes[:, P * k:P * (k + 1)].bitcast(FP8X4), scales[:, P * k:P * (k + 1)]) for k in range(width // P)]

        def quantize_mix(s, ix, ih):
            ops = quantize(mix[s], "mix", 0 if live(ix) else 2, 4 if live(ih) else 2)
            x_ops[ix], h_ops[ih] = ops[0:2], ops[2:4]


        def stage1(i):
            a = i // TILES
            for c in range(GP):
                s_ps[i, c] = psum.tile([P, KP], F32, name="s_ps%d" % c)
                for g in range(GE):
                    nc.tensor.matmul_mx(
                        out=s_ps[i, c][:],
                        lhsT=x_ops[i][g][0],
                        lhsT_scale=x_ops[i][g][1],
                        rhs=r_sb[a, g][:, 2 * KP * c:2 * KP * (c + 1)].bitcast(FP4X4),
                        rhs_scale=r_planes[a % 2][:, g, KP * c:KP * (c + 1)],
                        start=(g == 0),
                        stop=(g == GE - 1),
                    )

        def saturate(i):
            th[i] = work.tile([P, PX], F32, name="th")
            for c in range(GP):
                nc.scalar.activation(out=pixel_group(th[i], c), in_=to_pair_order(s_ps[i, c][:]), func=ACT.Tanh)

        def sort_gain(a, copy):
            gain_sorted[a] = work.tile([P, KP], F32, name="gain_sorted")
            copy(out=in_pair_order(gain_sorted[a][:]), in_=to_pair_order(gain_sb[a][:, 0:KP]))

        def new_third():
            fresh = work.tile([P, PX], BF16, name="third", align_bytes=64, bufs=4)
            return fresh

        def gain_first_group(eng, i):
            eng.tensor_tensor(out=h_bf[i][:, 0:KP], in0=th[i][:, 0:KP], in1=gain_sorted[i // TILES][:], op=ALU.mult)

        def gain_other_groups(i):
            nc.vector.tensor_tensor(
                out=in_pair_order(h_bf[i][:, KP:PX]),
                in0=in_pair_order(th[i][:, KP:PX]),
                in1=to_pair_order(gain_sb[i // TILES][:, KP:PX]),
                op=ALU.mult,
            )

        def gain_by_group(i):
            for c in range(GP):
                nc.vector.tensor_tensor(
                    out=pixel_group(h_bf[i], c),
                    in0=pixel_group(th[i], c),
                    in1=to_pair_order(gain_sb[i // TILES][:, KP * c:KP * (c + 1)]),
                    op=ALU.mult,
                )

        def turn_pairs(bank, slot, src, c):
            pairs = src[:].bitcast(F32)
            for u in range(2):
                first = P * u if c == 0 else 2 * P * (u + 1) + P * (c - 1)
                nc.tensor.transpose(bank[:, 2 * slot + u, :], pairs[:, first:first + P], ident[:])

        def copy_pairs(dst, bank, lo, hi):
            nc.scalar.copy(
                out=dst.bitcast(F32).rearrange("p (g r u) -> p g r u", r=P, u=2),
                in_=bank[:, 2 * lo:2 * hi, :].rearrange("p (g u) r -> p g r u", u=2),
            )

        def turn_h(s, i, tag_a, tag_b, bufs):
            bank_a[s] = psum.tile([P, 4, P], F32, name=tag_a, bufs=bufs)
            turn_pairs(bank_a[s], 0, h_bf[i], 0)
            turn_pairs(bank_a[s], 1, h_bf[i], 1)
            bank_b[s] = psum.tile([P, 4, P], F32, name=tag_b, bufs=bufs)
            turn_pairs(bank_b[s], 0, h_bf[i], 2)

        def copy_h(s):
            copy_pairs(mix[s][:, 2 * KP:4 * KP], bank_a[s], 0, 2)
            third[s] = new_third()
            copy_pairs(third[s][:, 0:KP], bank_b[s], 0, 1)

        def quantize_third(s, i):
            h_ops[i] = h_ops[i] + quantize(third[s][:, 0:KP], "third", 0, 1)


        def stage2(i, tag):
            a = i // TILES
            z_ps[i] = psum.tile([P, N], F32, name=tag)
            for g in range(GP):
                nc.tensor.matmul_mx(
                    out=z_ps[i][:],
                    lhsT=h_ops[i][g][0],
                    lhsT_scale=h_ops[i][g][1],
                    rhs=c_sb[a][:, g, :].bitcast(FP4X4),
                    rhs_scale=c_planes[a % 2][:, g, :],
                    start=(g == 0),
                    stop=(g == GP - 1),
                )

        def add_rest(i):
            offs[i] = work.tile([P, N], F32, name="offs")
            nc.vector.tensor_tensor(out=offs[i][:], in0=z_ps[i][:], in1=rest_sb[i // TILES][:], op=ALU.add)

        def apply_stiff(i):
            a, j = divmod(i, TILES)
            y_sb[i] = work.tile([P, N], F32, name="y_t", bufs=4)
            nc.vector.tensor_tensor(out=y_sb[i][:], in0=offs[i][:], in1=stiff_sb[a][:], op=ALU.mult)
            nc.sync.dma_start(out=out_0[a, j * P:(j + 1) * P, :], in_=y_sb[i][:])

        def round_y(i):
            y_bf[i] = work.tile([P, N], BF16, name="y_bf")
            nc.scalar.copy(out=in_pair_order(y_bf[i][:]), in_=to_pair_order(y_sb[i][:]))

        def apply_stiff_rounded(i):
            y_bf[i] = work.tile([P, N], BF16, name="y_bf")
            nc.vector.tensor_tensor(
                out=in_pair_order(y_bf[i][:]),
                in0=to_pair_order(offs[i][:]),
                in1=to_pair_order(stiff_sb[i // TILES][:]),
                op=ALU.mult,
            )

        def copy_y(i, bank, lo, hi):
            if i % 2 == 0:
                y_in[i // 2] = work.tile([P, 2 * KP], BF16, name="y_in", align_bytes=64)
            copy_pairs(y_in[i // 2][:, KP * (i % 2):KP * (i % 2 + hi - lo)], bank, lo, hi)

        def turn_and_copy_two_y(i, tag):
            bank = psum.tile([P, 4, P], F32, name=tag)
            turn_pairs(bank, 0, y_bf[i], 0)
            turn_pairs(bank, 1, y_bf[i + 1], 0)
            copy_y(i, bank, 0, 2)

        def quantize_y(i):
            a, j = divmod(i, TILES)
            if j == 0:
                y_scales[a] = work.tile([P, T], U8, name="y_scales", align_bytes=64)
            y_codes = work.tile([P, 2 * P], U32, name="y_codes", align_bytes=64)
            nc.vector.quantize_mx(
                out=y_codes[:].bitcast(FP8X4), scales=y_scales[a][:, P * j:P * (j + 2)], in_=y_in[i // 2][:]
            )
            nc.sync.dma_start(
                out=out_1[0, :, P * i:P * (i + 2), :].rearrange("p m t -> p (m t)").bitcast(I32),
                in_=y_codes[:].bitcast(I32),
            )
            if j + 2 == TILES:
                for q in range(4):
                    queue = nc.scalar if a == G - 1 and q % 2 == 1 else nc.sync
                    queue.dma_start(
                        out=out_2[0, 4 * q:4 * q + 4, T * a:T * (a + 1)].bitcast(I32),
                        in_=y_scales[a][32 * q:32 * q + 4, :].bitcast(I32),
                    )


        load_dv(0)
        vref_first = load_vref(0, 1)
        for i in range(1, AHEAD):
            load_dv(i)
        load_r(0)
        gain_sb[0] = load_row("gain_row", gain[0])
        load_dv(AHEAD)
        vref_others = load_vref(1, G)
        load_c(0)
        load_dv(AHEAD + 1)
        load_offsets(0)
        nc.vector.reciprocal(out=recip[:, 0:GE, :], in_=vref_first[:, :, 0:4])

        for i, (tag, bufs) in enumerate([("x_ps", 2), ("x_ps", 2), ("bank_a", 1), ("bank_b", 1)]):
            turn_x(i, tag, bufs)
            new_mix(i - 1)
            divide_x(i, i - 1)
            if i > 0:
                quantize_mix(i - 2, i - 1, NO_TILE)

        last = UNITS - 1
        for s in range(last):
            nxt, phase = s // TILES + 1, s % TILES
            if s > 0 and live(s + 5):
                load_dv(s + 5)
            if nxt < G and phase == 1:
                load_r(nxt)
            if nxt < G and phase == 2:
                gain_sb[nxt] = load_row("gain_row", gain[nxt])
            if nxt < G and phase == 3:
                load_c(nxt)
            if s > 0 and phase == 0:
                load_offsets(s // TILES)
            if s == AHEAD - 2:
                nc.vector.reciprocal(out=recip[:, GE:, :], in_=vref_others[:, :, 0:4])

            ix, ig, ih, iz, iy = s + 1, s - 1, s - 2, s - 3, s - 4
            shared = s - 1 in third
            if live(ih):
                turn_h(s, ih, "bank_a", "bank_b", 1)
            if AHEAD <= s + 2 < UNITS:
                turn_x(s + 2, "x_ps", 2)
            if live(iy):
                turn_pairs(bank_b[s], 1, y_bf[iy], 0)
            if live(ig):
                h_bf[ig] = third[s - 1] if shared else new_third()
            if shared:
                gain_first_group(nc.gpsimd, ig)
            if ix >= AHEAD:
                new_mix(s)
                divide_x(ix, s)
            if live(iz):
                add_rest(iz)
            if live(ih):
                copy_h(s)
            if live(iy):
                copy_y(iy, bank_b[s], 1, 2)
            if s > 0 and phase == 0:
                sort_gain(s // TILES, nc.scalar.copy)
            stage1(s)
            if shared:
                gain_other_groups(ig)
            elif live(ig):
                gain_by_group(ig)
            if ih == 0:
                sort_gain(0, nc.vector.tensor_copy)
            if live(iz):
                apply_stiff(iz)
            if live(ih):
                quantize_mix(s, ix, ih)
            if live(iy) and iy % 2 == 1:
                quantize_y(iy - 1)
            if live(ih):
                quantize_third(s, ih)
                stage2(ih, "z_ps")
            saturate(s)
            if live(iz):
                round_y(iz)

        a_tile, b_tile, c_tile = last - 2, last - 1, last
        s = last
        turn_h(s, a_tile, "bank_a", "bank_b", 1)
        turn_pairs(bank_b[s], 1, y_bf[last - 4], 0)
        stage1(c_tile)
        h_bf[b_tile] = new_third()
        gain_first_group(nc.vector, b_tile)
        gain_other_groups(b_tile)
        new_mix(s)
        copy_h(s)
        copy_y(last - 4, bank_b[s], 1, 2)
        add_rest(last - 3)
        quantize_mix(s, NO_TILE, a_tile)
        quantize_third(s, a_tile)
        saturate(c_tile)

        s = last + 1
        turn_h(s, b_tile, "x_ps", "x_ps", 2)
        stage2(a_tile, "z_ps")
        apply_stiff(last - 3)
        quantize_y(last - 5)
        new_mix(s)
        copy_h(s)
        h_bf[c_tile] = new_third()
        gain_by_group(c_tile)
        round_y(last - 3)
        quantize_mix(s, NO_TILE, b_tile)
        quantize_third(s, b_tile)
        add_rest(a_tile)

        s = last + 2
        turn_h(s, c_tile, "bank_a", "bank_b", 1)
        stage2(b_tile, "s_ps0")
        new_mix(s)
        copy_h(s)
        quantize_mix(s, NO_TILE, c_tile)
        apply_stiff(a_tile)
        round_y(a_tile)
        quantize_third(s, c_tile)
        stage2(c_tile, "s_ps1")

        turn_and_copy_two_y(last - 3, "bank_a")
        add_rest(b_tile)
        add_rest(c_tile)
        apply_stiff(b_tile)
        round_y(b_tile)
        apply_stiff_rounded(c_tile)
        quantize_y(last - 3)
        turn_and_copy_two_y(b_tile, "bank_b")
        apply_stiff(c_tile)
        quantize_y(b_tile)
